import numpy as np
import ml_dtypes


def mxq(x, axis, fmt="e4m3"):
    dtype, down = {"e4m3": (ml_dtypes.float8_e4m3fn, 7), "e5m2": (ml_dtypes.float8_e5m2, 14)}[fmt]
    v = np.moveaxis(np.asarray(x, np.float32).astype(ml_dtypes.bfloat16).astype(np.float64), axis, -1)
    blocks = v.reshape(v.shape[:-1] + (-1, 32))
    amax = np.abs(blocks).max(-1, keepdims=True)
    byte = np.maximum(np.where(amax > 0, np.frexp(amax)[1] - 1 + 127, 0) - down, 1)
    scale = np.exp2(byte - 127.0)
    codes = (blocks / scale).astype(np.float32).astype(dtype).astype(np.float64)
    return np.moveaxis((codes * scale).reshape(v.shape), -1, axis)


WIDE = False


def mx_kscale(k):
    if not WIDE:
        return np.ones(k)
    levels = np.array([10, -10, 5, -5, 0])
    if k % 512:
        return np.exp2(np.random.permutation(np.resize(levels, k // 32))).repeat(32)
    a = np.empty((k // 512, 16))
    for p in range(k // 512):
        a[p, :8] = np.random.permutation(np.resize(levels, 8))
        for g in range(8):
            far = levels[np.abs(levels - a[p, g]) >= 10]
            a[p, g + 8] = far[np.random.randint(len(far))]
    return np.exp2(a.ravel()).repeat(32)


def f64(x):
    return np.asarray(x).astype(np.float64)


def striped(idx):
    return np.tile(idx.reshape(-1, 16).T, (8, 1)).astype(np.uint16)


def unstriped(offs):
    return offs[:16].T.reshape(-1).astype(np.int64)


E2M1 = np.array([0.0, 0.5, 1.0, 1.5, 2.0, 3.0, 4.0, 6.0, -0.0, -0.5, -1.0, -1.5, -2.0, -3.0, -4.0, -6.0])


def pack_weight(w, fmt):
    k, n = w.shape
    w = f64(np.asarray(w, np.float32).astype(ml_dtypes.bfloat16)).reshape(k // 32, 32, n)
    amax = np.abs(w).max(1)
    if fmt == "e4m3":
        byte = np.frexp(amax)[1] - 1 + 127 - 7
    else:
        mant, ex = np.frexp(amax / 6.0)
        byte = np.where(mant > 0.5, ex, ex - 1) + 127
    byte = np.clip(np.where(amax > 0, byte, 1), 1, 254)
    scaled = (w * np.exp2(127.0 - byte)[:, None, :]).reshape(k, n).astype(np.float32)
    by_word = np.ascontiguousarray(scaled.reshape(k // 512, 128, 4, n).transpose(0, 1, 3, 2))
    if fmt == "e4m3":
        words = by_word.astype(ml_dtypes.float8_e4m3fn).view(np.uint8)
    else:
        c = by_word.astype(ml_dtypes.float4_e2m1fn).view(np.uint8) & 0xF
        words = (c[..., 0::2] | (c[..., 1::2] << 4)).reshape(k // 512, 128, 2 * n)
    return np.ascontiguousarray(words), np.ascontiguousarray(byte.astype(np.uint8).reshape(k // 512, 16, n))


def unpack_weight(words, scales, fmt):
    g, _, n = scales.shape
    words = np.ascontiguousarray(words).reshape(g, 128, n, -1)
    if fmt == "e4m3":
        vals = words.view(ml_dtypes.float8_e4m3fn).astype(np.float64)
    else:
        nib = np.empty((g, 128, n, 4), np.uint8)
        nib[..., 0::2] = words & 0xF
        nib[..., 1::2] = words >> 4
        vals = E2M1[nib]
    vals = vals * np.repeat(np.exp2(scales.astype(np.float64) - 127.0), 8, axis=1)[..., None]
    return vals.transpose(0, 1, 3, 2).reshape(g * 512, n)


def gelu(v):
    return 0.5 * v * (1.0 + np.tanh(np.sqrt(2.0 / np.pi) * (v + 0.044715 * v**3)))


K, KP, H, T, S, T2, S2, D = 2048, 1024, 512, 2048, 1024, 2048, 1024, 16


def setup_inputs():
    n = np.random.standard_normal
    s = mx_kscale(K)[:, None]
    u = mx_kscale(H)[:, None]
    idx = np.random.permutation(T)[:S]
    idx2 = np.random.permutation(T2)[:S2]
    a = n((K, D)) / np.sqrt(D)
    z = n((D, T))
    w = n((K, H)) / np.sqrt(K)
    b1 = 0.5 * n(H)
    m = w.T @ a
    points = m @ z[:, idx] + b1[:, None]
    anchors = m @ n((D, T2)) + b1[:, None]
    w = w / s * u.T
    tab_words, tab_scales = pack_weight((a @ z) * s, "e4m3")
    w4_words, w4_scales = pack_weight(w[KP:], "e2m1")
    tab2_words, tab2_scales = pack_weight(anchors / H / u, "e4m3")
    return {"tab_words": tab_words, "tab_scales": tab_scales, "offs": striped(idx),
            "tab2_words": tab2_words, "tab2_scales": tab2_scales, "offs2": striped(idx2),
            "w1": w[:KP].astype(np.float32), "w4_words": w4_words, "w4_scales": w4_scales,
            "b1": (b1 * u[:, 0]).astype(np.float32),
            "p2": ((points ** 2).sum(0) / H).astype(np.float32),
            "a2": ((anchors[:, idx2] ** 2).sum(0) / H).astype(np.float32)}


def reference(tab_words, tab_scales, offs, tab2_words, tab2_scales, offs2, w1, w4_words, w4_scales, b1, p2, a2):
    v = unpack_weight(tab_words, tab_scales, "e4m3")[:, unstriped(offs)]
    v2 = unpack_weight(tab2_words, tab2_scales, "e4m3")[:, unstriped(offs2)]
    w4 = unpack_weight(w4_words, w4_scales, "e2m1")
    h = mxq(f64(w1), 0, "e4m3").T @ v[:KP] + w4.T @ v[KP:]
    h = h + f64(b1)[:, None]
    dots = v2.T @ mxq(h, 0, "e4m3")
    y = 2 * dots - f64(p2)[None, :] - f64(a2)[:, None]
    return np.exp(y)

@@ -1,0 +1,233 @@
+from contextlib import ExitStack
+
+import concourse.mybir as mybir
+from concourse.masks import make_identity
+
+K, KP, H, T, S, S2 = 2048, 1024, 512, 2048, 1024, 1024
+FLOPS = 2 * K * H * S + 2 * H * S2 * S
+
+F32 = mybir.dt.float32
+BF16 = mybir.dt.bfloat16
+I32 = mybir.dt.int32
+U32 = mybir.dt.uint32
+U16 = mybir.dt.uint16
+U8 = mybir.dt.uint8
+FP8X4 = mybir.dt.float8_e4m3fn_x4
+FP4X4 = mybir.dt.float4_e2m1fn_x4
+ACT = mybir.ActivationFunctionType
+ALU = mybir.AluOpType
+
+P = 128
+PACK = 4
+N = 512
+HALVES = S // N
+PASSES = K // (P * PACK)
+W1_PASSES = KP // (P * PACK)
+ROW_TILES = S2 // P
+QUADS = 4
+BANKS = 8
+
+
+def tile_list_point_anchor_affinity_kernel(
+    tc, tab_words, tab_scales, offs, tab2_words, tab2_scales, offs2, w1, w4_words, w4_scales, b1, p2, a2, out
+):
+    nc = tc.nc
+    with ExitStack() as ctx:
+        lists = ctx.enter_context(tc.tile_pool(name="lists", bufs=1))
+        keep = ctx.enter_context(tc.tile_pool(name="keep", bufs=1))
+        ring = ctx.enter_context(tc.tile_pool(name="ring", bufs=4))
+        psum = ctx.enter_context(tc.psum_pool(name="psum", bufs=1))
+
+        def bank(b):
+            return psum.tile([P, N], F32, name="bank%d" % b)
+
+        def held(shape, dtype, name):
+            return keep.tile(shape, dtype, name=name, align_bytes=64)
+
+        anchor_list = lists.tile([P, S2 // 16], U16, name="anchor_list")
+        point_list = lists.tile([P, S // 16], U16, name="point_list")
+        nc.sync.dma_start(point_list[:], offs)
+        nc.sync.dma_start(anchor_list[:], offs2)
+
+        tab2_scale_win = held([P, T], U8, "tab2_scale_win")
+        tab_scale_win = held([P, T], U8, "tab_scale_win")
+        w4_scale_raw = held([P, 2, H], U8, "w4_scale_raw")
+        late_planes = held([P, 2, S], U8, "late_planes")
+        rows = held([P, P], F32, "rows")
+        nc.gpsimd.memset(tab_scale_win[:].bitcast(I32), 0)
+        nc.gpsimd.memset(rows[:], 0.0)
+        nc.vector.memset(w4_scale_raw[:].bitcast(I32), 0)
+        nc.vector.memset(tab2_scale_win[:].bitcast(I32), 0)
+        nc.vector.memset(late_planes[:].bitcast(I32), 0)
+        for q in range(QUADS):
+            nc.sync.dma_start(
+                tab_scale_win[32 * q : 32 * q + 16, :].bitcast(I32), tab_scales[:, 4 * q : 4 * q + 4, :].bitcast(I32)
+            )
+        bias = held([P, PACK], F32, "bias")
+        nc.gpsimd.dma_start(rows[0:ROW_TILES, :], a2.rearrange("(c n) -> c n", n=P))
+        nc.gpsimd.dma_start(rows[ROW_TILES : 2 * ROW_TILES, :], p2.rearrange("(c n) -> c n", n=P))
+        identity = held([P, P], F32, "identity")
+        make_identity(nc, identity[:])
+        for q in range(QUADS):
+            nc.gpsimd.dma_start(
+                w4_scale_raw[32 * q : 32 * q + 4, :, :].bitcast(I32),
+                w4_scales[:, 4 * q : 4 * q + 4, :].bitcast(I32).rearrange("a r e -> r a e"),
+            )
+
+        def load_words(src, name):
+            t = held([P, T], I32, name)
+            nc.sync.dma_start(t[:], src.rearrange("p t i -> p (t i)").bitcast(I32))
+            return t
+
+        def load_w1(a):
+            t = held([P, PACK, H], F32, "w1_raw%d" % a)
+            nc.sync.dma_start(t[:], w1[a * 512 : (a + 1) * 512, :].rearrange("(p j) c -> p j c", j=PACK))
+            return t
+
+        def move_plane(a, q):
+            nc.sync.dma_start(
+                late_planes[32 * q : 32 * q + 4, a - W1_PASSES, :].bitcast(I32),
+                point_scales[32 * q + 4 * a : 32 * q + 4 * a + 4, :].bitcast(I32),
+            )
+
+        point_scales = held([P, S], U8, "point_scales")
+        nc.vector.tensor_copy(point_scales[:], tab_scale_win[:].indirect(point_list[:]))
+
+        tab_win = [load_words(tab_words[0], "tab_win0")]
+        w1_raw = [load_w1(0)]
+        for q in range(QUADS):
+            nc.sync.dma_start(
+                tab2_scale_win[32 * q : 32 * q + 4, :].bitcast(I32), tab2_scales[0, 4 * q : 4 * q + 4, :].bitcast(I32)
+            )
+        w4_raw = held([P, 2, 2 * H], U8, "w4_raw")
+        nc.sync.dma_start(w4_raw[:].bitcast(I32), w4_words.bitcast(I32).rearrange("a p w -> p a w"))
+        nc.sync.dma_start(bias[:], b1.rearrange("(p t) -> p t", t=PACK))
+        w1_raw.append(load_w1(1))
+        tab_win.append(load_words(tab_words[1], "tab_win1"))
+        moves = [(a, q) for a in range(W1_PASSES, PASSES) for q in range(QUADS)]
+        for a, q in moves[:6]:
+            move_plane(a, q)
+        tab_win.append(load_words(tab_words[2], "tab_win2"))
+        for a, q in moves[6:]:
+            move_plane(a, q)
+        tab_win.append(load_words(tab_words[3], "tab_win3"))
+        tab2_win = load_words(tab2_words[0], "tab2_win")
+
+        turned = bank(4)
+        nc.tensor.transpose(turned[:, 0:P], rows[:], identity[:])
+        minus_cols = held([P, 2 * ROW_TILES], F32, "minus_cols")
+        nc.scalar.activation(minus_cols[:], turned[:, 0 : 2 * ROW_TILES], ACT.Copy, scale=-1.0)
+        minus_p2 = held([P, S], F32, "minus_p2")
+        for half in range(HALVES):
+            spread = bank(5 + half)
+            for c in range(N // P):
+                col = ROW_TILES + half * (N // P) + c
+                nc.tensor.transpose(
+                    spread[:, c * P : (c + 1) * P], minus_cols[:, col : col + 1].to_broadcast([P, P]), identity[:]
+                )
+            nc.scalar.copy(minus_p2[:, half * N : (half + 1) * N], spread[:])
+
+        point_words = {}
+
+        def gather_points(a, half):
+            g = held([P, N], U32, "point_words%d_%d" % (a, half))
+            cols = slice(half * N // 16, (half + 1) * N // 16)
+            nc.vector.tensor_copy(g[:], tab_win[a][:].bitcast(U32).indirect(point_list[:, cols]))
+            point_words[a, half] = g
+
+        for half in range(HALVES):
+            gather_points(0, half)
+
+        anchor_scales = held([P, S2], U8, "anchor_scales")
+        nc.vector.tensor_copy(anchor_scales[:], tab2_scale_win[:].indirect(anchor_list[:]))
+
+        w1_codes, w1_scales = [], []
+        for a in range(W1_PASSES):
+            grouped = held([P, PACK, P, PACK], BF16, "w1_grouped%d" % a)
+            nc.scalar.copy(
+                grouped[:].rearrange("p t m j -> p m j t"), w1_raw[a][:].rearrange("p j (m t) -> p m j t", t=PACK)
+            )
+            codes = held([P, H], U32, "w1_codes%d" % a)
+            scales = held([P, H], U8, "w1_scales%d" % a)
+            nc.vector.quantize_mx(codes[:].bitcast(FP8X4), scales[:], grouped[:].rearrange("p t m j -> p (t m j)"))
+            w1_codes.append(codes)
+            w1_scales.append(scales)
+
+        w4_codes = held([P, 2, 2 * H], U8, "w4_codes")
+        w4_planes = held([P, 2, H], U8, "w4_planes")
+        nc.vector.tensor_copy(
+            w4_codes[:].bitcast(U16).rearrange("p a (t m) -> p a m t", t=PACK),
+            w4_raw[:].bitcast(U16).rearrange("p a (m t) -> p a m t", t=PACK),
+        )
+        nc.vector.tensor_copy(
+            w4_planes[:].rearrange("p a (t m) -> p a m t", t=PACK),
+            w4_scale_raw[:].rearrange("p a (m t) -> p a m t", t=PACK),
+        )
+
+
+        h_banks = [[bank(PACK * half + t) for t in range(PACK)] for half in range(HALVES)]
+
+        def project(a, half):
+            cols = slice(half * N, (half + 1) * N)
+            for t in range(PACK):
+                if a < W1_PASSES:
+                    lhs = w1_codes[a][:, t * P : (t + 1) * P].bitcast(FP8X4)
+                    lhs_scale = w1_scales[a][:, t * P : (t + 1) * P]
+                    rhs_scale = point_scales[4 * a : P, cols]
+                else:
+                    lhs = w4_codes[:, a - W1_PASSES, 2 * t * P : 2 * (t + 1) * P].bitcast(FP4X4)
+                    lhs_scale = w4_planes[:, a - W1_PASSES, t * P : (t + 1) * P]
+                    rhs_scale = late_planes[:, a - W1_PASSES, cols]
+                nc.tensor.matmul_mx(
+                    h_banks[half][t][:],
+                    lhsT=lhs,
+                    lhsT_scale=lhs_scale,
+                    rhs=point_words[a, half][:].bitcast(FP8X4),
+                    rhs_scale=rhs_scale,
+                    start=(a == 0),
+                    stop=(a == PASSES - 1),
+                )
+
+        for a in range(PASSES):
+            for half in range(HALVES):
+                if a >= 1:
+                    gather_points(a, half)
+                project(a, half)
+
+        anchor_words = held([P, S2], U32, "anchor_words")
+        nc.vector.tensor_copy(anchor_words[:], tab2_win[:].bitcast(U32).indirect(anchor_list[:]))
+
+        h_codes, h_scales = [], []
+        for half in range(HALVES):
+            planes = held([P, PACK, N], BF16, "h_planes%d" % half)
+            for t in range(PACK):
+                nc.scalar.activation(planes[:, t, :], h_banks[half][t][:], ACT.Identity, bias=bias[:, t : t + 1])
+            grouped = held([P, N, PACK], BF16, "h_grouped%d" % half)
+            nc.vector.tensor_copy(
+                grouped[:].rearrange("p (c i) t -> p c t i", i=4), planes[:].rearrange("p t (c i) -> p c t i", i=4)
+            )
+            codes = held([P, N], U32, "h_codes%d" % half)
+            scales = held([P, N], U8, "h_scales%d" % half)
+            nc.vector.quantize_mx(codes[:].bitcast(FP8X4), scales[:], grouped[:].rearrange("p n t -> p (n t)"))
+            h_codes.append(codes)
+            h_scales.append(scales)
+
+        for half in range(HALVES):
+            cols = slice(half * N, (half + 1) * N)
+            for c in range(ROW_TILES):
+                anchors = slice(c * P, (c + 1) * P)
+                dots = bank((half * ROW_TILES + c) % BANKS)
+                nc.tensor.matmul_mx(
+                    dots[:],
+                    lhsT=anchor_words[:, anchors].bitcast(FP8X4),
+                    lhsT_scale=anchor_scales[:, anchors],
+                    rhs=h_codes[half][:].bitcast(FP8X4),
+                    rhs_scale=h_scales[half][:],
+                    start=True,
+                    stop=True,
+                )
+                exponent = ring.tile([P, N], F32, name="exponent")
+                nc.vector.scalar_tensor_tensor(exponent[:], dots[:], 2.0, minus_p2[:, cols], ALU.mult, ALU.add)
+                result = ring.tile([P, N], F32, name="result", bufs=10)
+                nc.scalar.activation(result[:], exponent[:], ACT.Exp, bias=minus_cols[:, c : c + 1])
+                nc.sync.dma_start(out[anchors, cols], result[:])

@@ -46,7 +46,6 @@ def tile_list_point_anchor_affinity_kernel(
 
         anchor_list = lists.tile([P, S2 // 16], U16, name="anchor_list")
         point_list = lists.tile([P, S // 16], U16, name="point_list")
-        nc.sync.dma_start(point_list[:], offs)
         nc.sync.dma_start(anchor_list[:], offs2)
 
         tab2_scale_win = held([P, T], U8, "tab2_scale_win")
@@ -54,24 +53,20 @@ def tile_list_point_anchor_affinity_kernel(
         w4_scale_raw = held([P, 2, H], U8, "w4_scale_raw")
         late_planes = held([P, 2, S], U8, "late_planes")
         rows = held([P, P], F32, "rows")
-        nc.gpsimd.memset(tab_scale_win[:].bitcast(I32), 0)
         nc.gpsimd.memset(rows[:], 0.0)
+        nc.gpsimd.memset(tab2_scale_win[:].bitcast(I32), 0)
+        nc.vector.memset(tab_scale_win[:].bitcast(I32), 0)
         nc.vector.memset(w4_scale_raw[:].bitcast(I32), 0)
-        nc.vector.memset(tab2_scale_win[:].bitcast(I32), 0)
         nc.vector.memset(late_planes[:].bitcast(I32), 0)
-        for q in range(QUADS):
-            nc.sync.dma_start(
-                tab_scale_win[32 * q : 32 * q + 16, :].bitcast(I32), tab_scales[:, 4 * q : 4 * q + 4, :].bitcast(I32)
-            )
-        bias = held([P, PACK], F32, "bias")
-        nc.gpsimd.dma_start(rows[0:ROW_TILES, :], a2.rearrange("(c n) -> c n", n=P))
-        nc.gpsimd.dma_start(rows[ROW_TILES : 2 * ROW_TILES, :], p2.rearrange("(c n) -> c n", n=P))
         identity = held([P, P], F32, "identity")
         make_identity(nc, identity[:])
+        bias = held([P, PACK], F32, "bias")
+        nc.gpsimd.dma_start(bias[:], b1.rearrange("(p t) -> p t", t=PACK))
+        nc.sync.dma_start(rows[0:ROW_TILES, :], a2.rearrange("(c n) -> c n", n=P))
+        nc.sync.dma_start(rows[ROW_TILES : 2 * ROW_TILES, :], p2.rearrange("(c n) -> c n", n=P))
         for q in range(QUADS):
-            nc.gpsimd.dma_start(
-                w4_scale_raw[32 * q : 32 * q + 4, :, :].bitcast(I32),
-                w4_scales[:, 4 * q : 4 * q + 4, :].bitcast(I32).rearrange("a r e -> r a e"),
+            nc.sync.dma_start(
+                tab2_scale_win[32 * q : 32 * q + 4, :].bitcast(I32), tab2_scales[0, 4 * q : 4 * q + 4, :].bitcast(I32)
             )
 
         def load_words(src, name):
@@ -90,27 +85,34 @@ def tile_list_point_anchor_affinity_kernel(
                 point_scales[32 * q + 4 * a : 32 * q + 4 * a + 4, :].bitcast(I32),
             )
 
+        tab_win = [load_words(tab_words[0], "tab_win0")]
+        nc.sync.dma_start(point_list[:], offs)
+        for q in range(QUADS):
+            nc.sync.dma_start(
+                tab_scale_win[32 * q : 32 * q + 16, :].bitcast(I32), tab_scales[:, 4 * q : 4 * q + 4, :].bitcast(I32)
+            )
+        w1_raw = [load_w1(a) for a in range(W1_PASSES)]
+        w4_raw = held([P, 2, 2 * H], U8, "w4_raw")
+        nc.sync.dma_start(w4_raw[:].bitcast(I32), w4_words.bitcast(I32).rearrange("a p w -> p a w"))
+        for q in range(QUADS):
+            nc.sync.dma_start(
+                w4_scale_raw[32 * q : 32 * q + 4, :, :].bitcast(I32),
+                w4_scales[:, 4 * q : 4 * q + 4, :].bitcast(I32).rearrange("a r e -> r a e"),
+            )
+        tab_win.append(load_words(tab_words[1], "tab_win1"))
+
+        anchor_scales = held([P, S2], U8, "anchor_scales")
+        nc.vector.tensor_copy(anchor_scales[:], tab2_scale_win[:].indirect(anchor_list[:]))
         point_scales = held([P, S], U8, "point_scales")
         nc.vector.tensor_copy(point_scales[:], tab_scale_win[:].indirect(point_list[:]))
 
-        tab_win = [load_words(tab_words[0], "tab_win0")]
-        w1_raw = [load_w1(0)]
-        for q in range(QUADS):
-            nc.sync.dma_start(
-                tab2_scale_win[32 * q : 32 * q + 4, :].bitcast(I32), tab2_scales[0, 4 * q : 4 * q + 4, :].bitcast(I32)
-            )
-        w4_raw = held([P, 2, 2 * H], U8, "w4_raw")
-        nc.sync.dma_start(w4_raw[:].bitcast(I32), w4_words.bitcast(I32).rearrange("a p w -> p a w"))
-        nc.sync.dma_start(bias[:], b1.rearrange("(p t) -> p t", t=PACK))
-        w1_raw.append(load_w1(1))
-        tab_win.append(load_words(tab_words[1], "tab_win1"))
         moves = [(a, q) for a in range(W1_PASSES, PASSES) for q in range(QUADS)]
+        tab_win.append(load_words(tab_words[2], "tab_win2"))
         for a, q in moves[:6]:
             move_plane(a, q)
-        tab_win.append(load_words(tab_words[2], "tab_win2"))
+        tab_win.append(load_words(tab_words[3], "tab_win3"))
         for a, q in moves[6:]:
             move_plane(a, q)
-        tab_win.append(load_words(tab_words[3], "tab_win3"))
         tab2_win = load_words(tab2_words[0], "tab2_win")
 
         turned = bank(4)
@@ -138,8 +140,6 @@ def tile_list_point_anchor_affinity_kernel(
         for half in range(HALVES):
             gather_points(0, half)
 
-        anchor_scales = held([P, S2], U8, "anchor_scales")
-        nc.vector.tensor_copy(anchor_scales[:], tab2_scale_win[:].indirect(anchor_list[:]))
 
         w1_codes, w1_scales = [], []
         for a in range(W1_PASSES):

@@ -26,6 +26,7 @@ W1_PASSES = KP // (P * PACK)
 ROW_TILES = S2 // P
 QUADS = 4
 BANKS = 8
+EARLY = 768
 
 
 def tile_list_point_anchor_affinity_kernel(
@@ -194,23 +195,46 @@ def tile_list_point_anchor_affinity_kernel(
                     gather_points(a, half)
                 project(a, half)
 
-        anchor_words = held([P, S2], U32, "anchor_words")
-        nc.vector.tensor_copy(anchor_words[:], tab2_win[:].bitcast(U32).indirect(anchor_list[:]))
+        early_words = held([P, EARLY], U32, "early_words")
+        nc.vector.tensor_copy(early_words[:], tab2_win[:].bitcast(U32).indirect(anchor_list[:, 0 : EARLY // 16]))
 
-        h_codes, h_scales = [], []
-        for half in range(HALVES):
+        def add_bias(half):
             planes = held([P, PACK, N], BF16, "h_planes%d" % half)
             for t in range(PACK):
                 nc.scalar.activation(planes[:, t, :], h_banks[half][t][:], ACT.Identity, bias=bias[:, t : t + 1])
-            grouped = held([P, N, PACK], BF16, "h_grouped%d" % half)
-            nc.vector.tensor_copy(
-                grouped[:].rearrange("p (c i) t -> p c t i", i=4), planes[:].rearrange("p t (c i) -> p c t i", i=4)
+            return planes
+
+        def quantize_h(grouped, half, cols):
+            nc.vector.quantize_mx(
+                h_codes[half][:, cols].bitcast(FP8X4), h_scales[half][:, cols], grouped[:].rearrange("p n t -> p (n t)")
             )
-            codes = held([P, N], U32, "h_codes%d" % half)
-            scales = held([P, N], U8, "h_scales%d" % half)
-            nc.vector.quantize_mx(codes[:].bitcast(FP8X4), scales[:], grouped[:].rearrange("p n t -> p (n t)"))
-            h_codes.append(codes)
-            h_scales.append(scales)
+
+        h_codes = [held([P, N], U32, "h_codes%d" % half) for half in range(HALVES)]
+        h_scales = [held([P, N], U8, "h_scales%d" % half) for half in range(HALVES)]
+
+        planes = add_bias(0)
+        parts = [slice(0, N // 2), slice(N // 2, N)]
+        grouped = [held([P, N // 2, PACK], BF16, "shared%d" % i) for i in range(2)]
+        for i in range(2):
+            nc.vector.tensor_copy(
+                grouped[i][:].rearrange("p (c i) t -> p c t i", i=4),
+                planes[:, :, parts[i]].rearrange("p t (c i) -> p c t i", i=4),
+            )
+        for i in range(2):
+            quantize_h(grouped[i], 0, parts[i])
+
+        late_words = held([P, S2 - EARLY], U32, "shared0")
+        nc.vector.tensor_copy(late_words[:], tab2_win[:].bitcast(U32).indirect(anchor_list[:, EARLY // 16 : S2 // 16]))
+
+        planes = add_bias(1)
+        grouped = held([P, N, PACK], BF16, "shared1")
+        nc.gpsimd.tensor_scalar(grouped[:], planes[:].rearrange("p t n -> p n t"), 1.0, 0.0, ALU.mult, ALU.add)
+        quantize_h(grouped, 1, slice(0, N))
+
+        def anchor_words(c):
+            if c * P < EARLY:
+                return early_words[:, c * P : (c + 1) * P]
+            return late_words[:, c * P - EARLY : (c + 1) * P - EARLY]
 
         for half in range(HALVES):
             cols = slice(half * N, (half + 1) * N)
@@ -219,7 +243,7 @@ def tile_list_point_anchor_affinity_kernel(
                 dots = bank((half * ROW_TILES + c) % BANKS)
                 nc.tensor.matmul_mx(
                     dots[:],
-                    lhsT=anchor_words[:, anchors].bitcast(FP8X4),
+                    lhsT=anchor_words(c).bitcast(FP8X4),
                     lhsT_scale=anchor_scales[:, anchors],
                     rhs=h_codes[half][:].bitcast(FP8X4),
                     rhs_scale=h_scales[half][:],

@@ -27,6 +27,7 @@ ROW_TILES = S2 // P
 QUADS = 4
 BANKS = 8
 EARLY = 768
+PASS_ORDER = (2, 3, 0, 1)
 
 
 def tile_list_point_anchor_affinity_kernel(
@@ -47,74 +48,65 @@ def tile_list_point_anchor_affinity_kernel(
 
         anchor_list = lists.tile([P, S2 // 16], U16, name="anchor_list")
         point_list = lists.tile([P, S // 16], U16, name="point_list")
-        nc.sync.dma_start(anchor_list[:], offs2)
+        nc.sync.dma_start(point_list[:], offs)
 
-        tab2_scale_win = held([P, T], U8, "tab2_scale_win")
-        tab_scale_win = held([P, T], U8, "tab_scale_win")
+        tab_scale_win = held([P, T], U8, "scale_win")
         w4_scale_raw = held([P, 2, H], U8, "w4_scale_raw")
-        late_planes = held([P, 2, S], U8, "late_planes")
+        planes_of = {a: held([P, S], U8, "plane%d" % a) for a in (2, 3, 0)}
         rows = held([P, P], F32, "rows")
+        nc.gpsimd.memset(w4_scale_raw[:].bitcast(I32), 0)
+        for q in range(QUADS):
+            nc.vector.memset(tab_scale_win[32 * q : 32 * q + 16, :].bitcast(I32), 0)
+        for a in (2, 3, 0):
+            nc.vector.memset(planes_of[a][:].bitcast(I32), 0)
         nc.gpsimd.memset(rows[:], 0.0)
-        nc.gpsimd.memset(tab2_scale_win[:].bitcast(I32), 0)
-        nc.vector.memset(tab_scale_win[:].bitcast(I32), 0)
-        nc.vector.memset(w4_scale_raw[:].bitcast(I32), 0)
-        nc.vector.memset(late_planes[:].bitcast(I32), 0)
+        nc.gpsimd.dma_start(rows[0:ROW_TILES, :], a2.rearrange("(c n) -> c n", n=P))
+        nc.gpsimd.dma_start(rows[ROW_TILES : 2 * ROW_TILES, :], p2.rearrange("(c n) -> c n", n=P))
         identity = held([P, P], F32, "identity")
         make_identity(nc, identity[:])
         bias = held([P, PACK], F32, "bias")
         nc.gpsimd.dma_start(bias[:], b1.rearrange("(p t) -> p t", t=PACK))
-        nc.sync.dma_start(rows[0:ROW_TILES, :], a2.rearrange("(c n) -> c n", n=P))
-        nc.sync.dma_start(rows[ROW_TILES : 2 * ROW_TILES, :], p2.rearrange("(c n) -> c n", n=P))
-        for q in range(QUADS):
-            nc.sync.dma_start(
-                tab2_scale_win[32 * q : 32 * q + 4, :].bitcast(I32), tab2_scales[0, 4 * q : 4 * q + 4, :].bitcast(I32)
-            )
 
         def load_words(src, name):
             t = held([P, T], I32, name)
             nc.sync.dma_start(t[:], src.rearrange("p t i -> p (t i)").bitcast(I32))
             return t
 
-        def load_w1(a):
-            t = held([P, PACK, H], F32, "w1_raw%d" % a)
+        def load_w1(a, name):
+            t = held([P, PACK, H], F32, name)
             nc.sync.dma_start(t[:], w1[a * 512 : (a + 1) * 512, :].rearrange("(p j) c -> p j c", j=PACK))
             return t
 
-        def move_plane(a, q):
-            nc.sync.dma_start(
-                late_planes[32 * q : 32 * q + 4, a - W1_PASSES, :].bitcast(I32),
-                point_scales[32 * q + 4 * a : 32 * q + 4 * a + 4, :].bitcast(I32),
-            )
-
-        tab_win = [load_words(tab_words[0], "tab_win0")]
-        nc.sync.dma_start(point_list[:], offs)
         for q in range(QUADS):
             nc.sync.dma_start(
-                tab_scale_win[32 * q : 32 * q + 16, :].bitcast(I32), tab_scales[:, 4 * q : 4 * q + 4, :].bitcast(I32)
+                tab_scale_win[32 * q + 16 : 32 * q + 32, :].bitcast(I32),
+                tab_scales[:, 4 * q : 4 * q + 4, :].bitcast(I32),
             )
-        w1_raw = [load_w1(a) for a in range(W1_PASSES)]
-        w4_raw = held([P, 2, 2 * H], U8, "w4_raw")
+        tab_win = {2: load_words(tab_words[2], "slot_a")}
+        tab_win[3] = load_words(tab_words[3], "slot_b")
+        w4_raw = held([P, 2, 2 * H], U8, "slot_c")
         nc.sync.dma_start(w4_raw[:].bitcast(I32), w4_words.bitcast(I32).rearrange("a p w -> p a w"))
+        nc.sync.dma_start(anchor_list[:], offs2)
         for q in range(QUADS):
             nc.sync.dma_start(
                 w4_scale_raw[32 * q : 32 * q + 4, :, :].bitcast(I32),
                 w4_scales[:, 4 * q : 4 * q + 4, :].bitcast(I32).rearrange("a r e -> r a e"),
             )
-        tab_win.append(load_words(tab_words[1], "tab_win1"))
+        w1_raw = [load_w1(0, "slot_d")]
 
-        anchor_scales = held([P, S2], U8, "anchor_scales")
-        nc.vector.tensor_copy(anchor_scales[:], tab2_scale_win[:].indirect(anchor_list[:]))
         point_scales = held([P, S], U8, "point_scales")
         nc.vector.tensor_copy(point_scales[:], tab_scale_win[:].indirect(point_list[:]))
-
-        moves = [(a, q) for a in range(W1_PASSES, PASSES) for q in range(QUADS)]
-        tab_win.append(load_words(tab_words[2], "tab_win2"))
-        for a, q in moves[:6]:
-            move_plane(a, q)
-        tab_win.append(load_words(tab_words[3], "tab_win3"))
-        for a, q in moves[6:]:
-            move_plane(a, q)
-        tab2_win = load_words(tab2_words[0], "tab2_win")
+        for a, span, queue in ((2, 100, nc.sync), (3, 100, nc.sync), (0, 104, nc.gpsimd)):
+            queue.dma_start(
+                planes_of[a][0:span, :].bitcast(I32),
+                point_scales[16 + 4 * a : 16 + 4 * a + span, :].bitcast(I32),
+            )
+        tab2_scale_win = held([P, T], U8, "scale_win")
+        nc.vector.memset(tab2_scale_win[:].bitcast(I32), 0)
+        for q in range(QUADS):
+            nc.sync.dma_start(
+                tab2_scale_win[32 * q : 32 * q + 4, :].bitcast(I32), tab2_scales[0, 4 * q : 4 * q + 4, :].bitcast(I32)
+            )
 
         turned = bank(4)
         nc.tensor.transpose(turned[:, 0:P], rows[:], identity[:])
@@ -133,27 +125,17 @@ def tile_list_point_anchor_affinity_kernel(
         point_words = {}
 
         def gather_points(a, half):
-            g = held([P, N], U32, "point_words%d_%d" % (a, half))
+            g = held([P, N], U32, "scale_win" if (a, half) == (0, 0) else "point_words%d_%d" % (a, half))
             cols = slice(half * N // 16, (half + 1) * N // 16)
             nc.vector.tensor_copy(g[:], tab_win[a][:].bitcast(U32).indirect(point_list[:, cols]))
             point_words[a, half] = g
 
         for half in range(HALVES):
-            gather_points(0, half)
+            gather_points(PASS_ORDER[0], half)
+        tab_win[0] = load_words(tab_words[0], "slot_a")
 
-
-        w1_codes, w1_scales = [], []
-        for a in range(W1_PASSES):
-            grouped = held([P, PACK, P, PACK], BF16, "w1_grouped%d" % a)
-            nc.scalar.copy(
-                grouped[:].rearrange("p t m j -> p m j t"), w1_raw[a][:].rearrange("p j (m t) -> p m j t", t=PACK)
-            )
-            codes = held([P, H], U32, "w1_codes%d" % a)
-            scales = held([P, H], U8, "w1_scales%d" % a)
-            nc.vector.quantize_mx(codes[:].bitcast(FP8X4), scales[:], grouped[:].rearrange("p t m j -> p (t m j)"))
-            w1_codes.append(codes)
-            w1_scales.append(scales)
-
+        for half in range(HALVES):
+            gather_points(PASS_ORDER[1], half)
         w4_codes = held([P, 2, 2 * H], U8, "w4_codes")
         w4_planes = held([P, 2, H], U8, "w4_planes")
         nc.vector.tensor_copy(
@@ -166,6 +148,25 @@ def tile_list_point_anchor_affinity_kernel(
         )
 
 
+        w1_raw.append(load_w1(1, "slot_b"))
+        tab_win[1] = load_words(tab_words[1], "slot_c")
+        anchor_scales = held([P, S2], U8, "anchor_scales")
+        nc.vector.tensor_copy(anchor_scales[:], tab2_scale_win[:].indirect(anchor_list[:]))
+
+        w1_codes, w1_scales = [], []
+        for a in range(W1_PASSES):
+            grouped = held([P, PACK, P, PACK], BF16, "w1_grouped%d" % a)
+            nc.scalar.copy(
+                grouped[:].rearrange("p t m j -> p m j t"), w1_raw[a][:].rearrange("p j (m t) -> p m j t", t=PACK)
+            )
+            if a == 0:
+                tab2_win = load_words(tab2_words[0], "slot_d")
+            codes = held([P, H], U32, "w1_codes%d" % a)
+            scales = held([P, H], U8, "w1_scales%d" % a)
+            nc.vector.quantize_mx(codes[:].bitcast(FP8X4), scales[:], grouped[:].rearrange("p t m j -> p (t m j)"))
+            w1_codes.append(codes)
+            w1_scales.append(scales)
+
         h_banks = [[bank(PACK * half + t) for t in range(PACK)] for half in range(HALVES)]
 
         def project(a, half):
@@ -174,24 +175,24 @@ def tile_list_point_anchor_affinity_kernel(
                 if a < W1_PASSES:
                     lhs = w1_codes[a][:, t * P : (t + 1) * P].bitcast(FP8X4)
                     lhs_scale = w1_scales[a][:, t * P : (t + 1) * P]
-                    rhs_scale = point_scales[4 * a : P, cols]
+                    rhs_scale = planes_of[0][4 * a : P, cols]
                 else:
                     lhs = w4_codes[:, a - W1_PASSES, 2 * t * P : 2 * (t + 1) * P].bitcast(FP4X4)
                     lhs_scale = w4_planes[:, a - W1_PASSES, t * P : (t + 1) * P]
-                    rhs_scale = late_planes[:, a - W1_PASSES, cols]
+                    rhs_scale = planes_of[a][:, cols]
                 nc.tensor.matmul_mx(
                     h_banks[half][t][:],
                     lhsT=lhs,
                     lhsT_scale=lhs_scale,
                     rhs=point_words[a, half][:].bitcast(FP8X4),
                     rhs_scale=rhs_scale,
-                    start=(a == 0),
-                    stop=(a == PASSES - 1),
+                    start=(a == PASS_ORDER[0]),
+                    stop=(a == PASS_ORDER[-1]),
                 )
 
-        for a in range(PASSES):
+        for a in PASS_ORDER:
             for half in range(HALVES):
-                if a >= 1:
+                if a < W1_PASSES:
                     gather_points(a, half)
                 project(a, half)
 

@@ -252,7 +252,7 @@ def tile_list_point_anchor_affinity_kernel(
                     stop=True,
                 )
                 exponent = ring.tile([P, N], F32, name="exponent")
-                nc.vector.scalar_tensor_tensor(exponent[:], dots[:], 2.0, minus_p2[:, cols], ALU.mult, ALU.add)
+                nc.vector.scalar_tensor_tensor(exponent[:], minus_p2[:, cols], 0.5, dots[:], ALU.mult, ALU.add)
                 result = ring.tile([P, N], F32, name="result", bufs=10)
-                nc.scalar.activation(result[:], exponent[:], ACT.Exp, bias=minus_cols[:, c : c + 1])
+                nc.scalar.activation(result[:], exponent[:], ACT.Exp, bias=minus_cols[:, c : c + 1], scale=2.0)
                 nc.sync.dma_start(out[anchors, cols], result[:])

@@ -27,7 +27,7 @@ ROW_TILES = S2 // P
 QUADS = 4
 BANKS = 8
 EARLY = 768
-PASS_ORDER = (2, 3, 0, 1)
+PASS_ORDER = (0, 1, 2, 3)
 
 
 def tile_list_point_anchor_affinity_kernel(
@@ -48,24 +48,24 @@ def tile_list_point_anchor_affinity_kernel(
 
         anchor_list = lists.tile([P, S2 // 16], U16, name="anchor_list")
         point_list = lists.tile([P, S // 16], U16, name="point_list")
+        bias = held([P, PACK], F32, "bias")
+        nc.sync.dma_start(anchor_list[:], offs2)
         nc.sync.dma_start(point_list[:], offs)
+        nc.sync.dma_start(bias[:], b1.rearrange("(p t) -> p t", t=PACK))
 
-        tab_scale_win = held([P, T], U8, "scale_win")
+        tab2_scale_win = held([P, T], U8, "tab2_scale_win")
+        tab_scale_win = held([P, T], U8, "slot_a")
         w4_scale_raw = held([P, 2, H], U8, "w4_scale_raw")
-        planes_of = {a: held([P, S], U8, "plane%d" % a) for a in (2, 3, 0)}
+        planes_of = {a: held([P, S], U8, "plane%d" % a) for a in (2, 3)}
         rows = held([P, P], F32, "rows")
-        nc.gpsimd.memset(w4_scale_raw[:].bitcast(I32), 0)
-        for q in range(QUADS):
-            nc.vector.memset(tab_scale_win[32 * q : 32 * q + 16, :].bitcast(I32), 0)
-        for a in (2, 3, 0):
-            nc.vector.memset(planes_of[a][:].bitcast(I32), 0)
-        nc.gpsimd.memset(rows[:], 0.0)
-        nc.gpsimd.dma_start(rows[0:ROW_TILES, :], a2.rearrange("(c n) -> c n", n=P))
-        nc.gpsimd.dma_start(rows[ROW_TILES : 2 * ROW_TILES, :], p2.rearrange("(c n) -> c n", n=P))
+        nc.vector.memset(tab2_scale_win[:].bitcast(I32), 0)
+        nc.vector.memset(tab_scale_win[:].bitcast(I32), 0)
+        nc.vector.memset(rows[:], 0.0)
+        nc.vector.memset(w4_scale_raw[:].bitcast(I32), 0)
+        for a in (2, 3):
+            nc.vector.memset(planes_of[a][96:P, :].bitcast(I32), 0)
         identity = held([P, P], F32, "identity")
         make_identity(nc, identity[:])
-        bias = held([P, PACK], F32, "bias")
-        nc.gpsimd.dma_start(bias[:], b1.rearrange("(p t) -> p t", t=PACK))
 
         def load_words(src, name):
             t = held([P, T], I32, name)
@@ -79,34 +79,51 @@ def tile_list_point_anchor_affinity_kernel(
 
         for q in range(QUADS):
             nc.sync.dma_start(
-                tab_scale_win[32 * q + 16 : 32 * q + 32, :].bitcast(I32),
+                tab2_scale_win[32 * q : 32 * q + 4, :].bitcast(I32), tab2_scales[0, 4 * q : 4 * q + 4, :].bitcast(I32)
+            )
+        w1_raw = [load_w1(0, "w1_raw0")]
+        for q in range(QUADS):
+            nc.sync.dma_start(
+                tab_scale_win[32 * q : 32 * q + 16, :].bitcast(I32),
                 tab_scales[:, 4 * q : 4 * q + 4, :].bitcast(I32),
             )
-        tab_win = {2: load_words(tab_words[2], "slot_a")}
-        tab_win[3] = load_words(tab_words[3], "slot_b")
-        w4_raw = held([P, 2, 2 * H], U8, "slot_c")
+        w1_raw.append(load_w1(1, "slot_b"))
+        nc.sync.dma_start(rows[0:ROW_TILES, :], a2.rearrange("(c n) -> c n", n=P))
+        nc.sync.dma_start(rows[ROW_TILES : 2 * ROW_TILES, :], p2.rearrange("(c n) -> c n", n=P))
+        tab_win = {a: load_words(tab_words[a], "tab_win%d" % a) for a in (0, 1)}
+        w4_raw = held([P, 2, 2 * H], U8, "w4_raw")
         nc.sync.dma_start(w4_raw[:].bitcast(I32), w4_words.bitcast(I32).rearrange("a p w -> p a w"))
-        nc.sync.dma_start(anchor_list[:], offs2)
         for q in range(QUADS):
             nc.sync.dma_start(
                 w4_scale_raw[32 * q : 32 * q + 4, :, :].bitcast(I32),
                 w4_scales[:, 4 * q : 4 * q + 4, :].bitcast(I32).rearrange("a r e -> r a e"),
             )
-        w1_raw = [load_w1(0, "slot_d")]
+        tab_win[2] = load_words(tab_words[2], "tab_win2")
 
+        anchor_scales = held([P, S2], U8, "anchor_scales")
+        nc.vector.tensor_copy(anchor_scales[:], tab2_scale_win[:].indirect(anchor_list[:]))
         point_scales = held([P, S], U8, "point_scales")
         nc.vector.tensor_copy(point_scales[:], tab_scale_win[:].indirect(point_list[:]))
-        for a, span, queue in ((2, 100, nc.sync), (3, 100, nc.sync), (0, 104, nc.gpsimd)):
-            queue.dma_start(
-                planes_of[a][0:span, :].bitcast(I32),
-                point_scales[16 + 4 * a : 16 + 4 * a + span, :].bitcast(I32),
-            )
-        tab2_scale_win = held([P, T], U8, "scale_win")
-        nc.vector.memset(tab2_scale_win[:].bitcast(I32), 0)
-        for q in range(QUADS):
-            nc.sync.dma_start(
-                tab2_scale_win[32 * q : 32 * q + 4, :].bitcast(I32), tab2_scales[0, 4 * q : 4 * q + 4, :].bitcast(I32)
-            )
+        for a in (2, 3):
+            nc.sync.dma_start(planes_of[a][0:100, :].bitcast(I32), point_scales[4 * a : 4 * a + 100, :].bitcast(I32))
+        tab_win[3] = load_words(tab_words[3], "slot_a")
+
+        w1_codes, w1_scales = [], []
+        for a in range(W1_PASSES):
+            grouped = held([P, PACK, P, PACK], BF16, "w1_grouped%d" % a)
+            dst = grouped[:].rearrange("p t m j -> p m j t")
+            src = w1_raw[a][:].rearrange("p j (m t) -> p m j t", t=PACK)
+            if a == 0:
+                nc.scalar.copy(dst, src)
+            else:
+                nc.scalar.copy(dst[:, 0 : P // 2], src[:, 0 : P // 2])
+                nc.vector.tensor_copy(dst[:, P // 2 : P], src[:, P // 2 : P])
+            codes = held([P, H], U32, "w1_codes%d" % a)
+            scales = held([P, H], U8, "w1_scales%d" % a)
+            nc.vector.quantize_mx(codes[:].bitcast(FP8X4), scales[:], grouped[:].rearrange("p t m j -> p (t m j)"))
+            w1_codes.append(codes)
+            w1_scales.append(scales)
+        tab2_win = load_words(tab2_words[0], "slot_b")
 
         turned = bank(4)
         nc.tensor.transpose(turned[:, 0:P], rows[:], identity[:])
@@ -125,47 +142,23 @@ def tile_list_point_anchor_affinity_kernel(
         point_words = {}
 
         def gather_points(a, half):
-            g = held([P, N], U32, "scale_win" if (a, half) == (0, 0) else "point_words%d_%d" % (a, half))
+            g = held([P, N], U32, "point_words%d_%d" % (a, half))
             cols = slice(half * N // 16, (half + 1) * N // 16)
             nc.vector.tensor_copy(g[:], tab_win[a][:].bitcast(U32).indirect(point_list[:, cols]))
             point_words[a, half] = g
 
-        for half in range(HALVES):
-            gather_points(PASS_ORDER[0], half)
-        tab_win[0] = load_words(tab_words[0], "slot_a")
-
-        for half in range(HALVES):
-            gather_points(PASS_ORDER[1], half)
         w4_codes = held([P, 2, 2 * H], U8, "w4_codes")
         w4_planes = held([P, 2, H], U8, "w4_planes")
-        nc.vector.tensor_copy(
-            w4_codes[:].bitcast(U16).rearrange("p a (t m) -> p a m t", t=PACK),
-            w4_raw[:].bitcast(U16).rearrange("p a (m t) -> p a m t", t=PACK),
-        )
-        nc.vector.tensor_copy(
-            w4_planes[:].rearrange("p a (t m) -> p a m t", t=PACK),
-            w4_scale_raw[:].rearrange("p a (m t) -> p a m t", t=PACK),
-        )
 
-
-        w1_raw.append(load_w1(1, "slot_b"))
-        tab_win[1] = load_words(tab_words[1], "slot_c")
-        anchor_scales = held([P, S2], U8, "anchor_scales")
-        nc.vector.tensor_copy(anchor_scales[:], tab2_scale_win[:].indirect(anchor_list[:]))
-
-        w1_codes, w1_scales = [], []
-        for a in range(W1_PASSES):
-            grouped = held([P, PACK, P, PACK], BF16, "w1_grouped%d" % a)
+        def deal_w4():
             nc.scalar.copy(
-                grouped[:].rearrange("p t m j -> p m j t"), w1_raw[a][:].rearrange("p j (m t) -> p m j t", t=PACK)
+                w4_codes[:].bitcast(U16).rearrange("p a (t m) -> p a m t", t=PACK),
+                w4_raw[:].bitcast(U16).rearrange("p a (m t) -> p a m t", t=PACK),
             )
-            if a == 0:
-                tab2_win = load_words(tab2_words[0], "slot_d")
-            codes = held([P, H], U32, "w1_codes%d" % a)
-            scales = held([P, H], U8, "w1_scales%d" % a)
-            nc.vector.quantize_mx(codes[:].bitcast(FP8X4), scales[:], grouped[:].rearrange("p t m j -> p (t m j)"))
-            w1_codes.append(codes)
-            w1_scales.append(scales)
+            nc.vector.tensor_copy(
+                w4_planes[:].rearrange("p a (t m) -> p a m t", t=PACK),
+                w4_scale_raw[:].rearrange("p a (m t) -> p a m t", t=PACK),
+            )
 
         h_banks = [[bank(PACK * half + t) for t in range(PACK)] for half in range(HALVES)]
 
@@ -175,7 +168,7 @@ def tile_list_point_anchor_affinity_kernel(
                 if a < W1_PASSES:
                     lhs = w1_codes[a][:, t * P : (t + 1) * P].bitcast(FP8X4)
                     lhs_scale = w1_scales[a][:, t * P : (t + 1) * P]
-                    rhs_scale = planes_of[0][4 * a : P, cols]
+                    rhs_scale = point_scales[4 * a : P, cols]
                 else:
                     lhs = w4_codes[:, a - W1_PASSES, 2 * t * P : 2 * (t + 1) * P].bitcast(FP4X4)
                     lhs_scale = w4_planes[:, a - W1_PASSES, t * P : (t + 1) * P]
@@ -191,9 +184,10 @@ def tile_list_point_anchor_affinity_kernel(
                 )
 
         for a in PASS_ORDER:
+            if a == W1_PASSES:
+                deal_w4()
             for half in range(HALVES):
-                if a < W1_PASSES:
-                    gather_points(a, half)
+                gather_points(a, half)
                 project(a, half)
 
         early_words = held([P, EARLY], U32, "early_words")

@@ -27,7 +27,6 @@ ROW_TILES = S2 // P
 QUADS = 4
 BANKS = 8
 EARLY = 768
-PASS_ORDER = (0, 1, 2, 3)
 
 
 def tile_list_point_anchor_affinity_kernel(
@@ -38,6 +37,7 @@ def tile_list_point_anchor_affinity_kernel(
         lists = ctx.enter_context(tc.tile_pool(name="lists", bufs=1))
         keep = ctx.enter_context(tc.tile_pool(name="keep", bufs=1))
         ring = ctx.enter_context(tc.tile_pool(name="ring", bufs=4))
+        laid = ctx.enter_context(tc.tile_pool(name="laid", bufs=1))
         psum = ctx.enter_context(tc.psum_pool(name="psum", bufs=1))
 
         def bank(b):
@@ -54,18 +54,23 @@ def tile_list_point_anchor_affinity_kernel(
         nc.sync.dma_start(bias[:], b1.rearrange("(p t) -> p t", t=PACK))
 
         tab2_scale_win = held([P, T], U8, "tab2_scale_win")
-        tab_scale_win = held([P, T], U8, "slot_a")
+        tab_scale_win = laid.tile([P, T], U8, name="tab_scale_win", align_bytes=64, offset=4 * H - 64)
         w4_scale_raw = held([P, 2, H], U8, "w4_scale_raw")
         planes_of = {a: held([P, S], U8, "plane%d" % a) for a in (2, 3)}
         rows = held([P, P], F32, "rows")
         nc.vector.memset(tab2_scale_win[:].bitcast(I32), 0)
-        nc.vector.memset(tab_scale_win[:].bitcast(I32), 0)
         nc.vector.memset(rows[:], 0.0)
         nc.vector.memset(w4_scale_raw[:].bitcast(I32), 0)
         for a in (2, 3):
             nc.vector.memset(planes_of[a][96:P, :].bitcast(I32), 0)
+        nc.gpsimd.memset(tab_scale_win[:].bitcast(I32), 0)
         identity = held([P, P], F32, "identity")
         make_identity(nc, identity[:])
+        for q in range(QUADS):
+            nc.gpsimd.dma_start(
+                tab_scale_win[32 * q : 32 * q + 16, :].bitcast(I32),
+                tab_scales[:, 4 * q : 4 * q + 4, :].bitcast(I32),
+            )
 
         def load_words(src, name):
             t = held([P, T], I32, name)
@@ -81,16 +86,11 @@ def tile_list_point_anchor_affinity_kernel(
             nc.sync.dma_start(
                 tab2_scale_win[32 * q : 32 * q + 4, :].bitcast(I32), tab2_scales[0, 4 * q : 4 * q + 4, :].bitcast(I32)
             )
-        w1_raw = [load_w1(0, "w1_raw0")]
-        for q in range(QUADS):
-            nc.sync.dma_start(
-                tab_scale_win[32 * q : 32 * q + 16, :].bitcast(I32),
-                tab_scales[:, 4 * q : 4 * q + 4, :].bitcast(I32),
-            )
-        w1_raw.append(load_w1(1, "slot_b"))
+        w1_raw = [load_w1(0, "slot_a")]
+        tab_win = {0: load_words(tab_words[0], "slot_c")}
         nc.sync.dma_start(rows[0:ROW_TILES, :], a2.rearrange("(c n) -> c n", n=P))
         nc.sync.dma_start(rows[ROW_TILES : 2 * ROW_TILES, :], p2.rearrange("(c n) -> c n", n=P))
-        tab_win = {a: load_words(tab_words[a], "tab_win%d" % a) for a in (0, 1)}
+        w1_raw.append(load_w1(1, "w1_raw1"))
         w4_raw = held([P, 2, 2 * H], U8, "w4_raw")
         nc.sync.dma_start(w4_raw[:].bitcast(I32), w4_words.bitcast(I32).rearrange("a p w -> p a w"))
         for q in range(QUADS):
@@ -98,7 +98,7 @@ def tile_list_point_anchor_affinity_kernel(
                 w4_scale_raw[32 * q : 32 * q + 4, :, :].bitcast(I32),
                 w4_scales[:, 4 * q : 4 * q + 4, :].bitcast(I32).rearrange("a r e -> r a e"),
             )
-        tab_win[2] = load_words(tab_words[2], "tab_win2")
+        tab_win[1] = load_words(tab_words[1], "slot_b")
 
         anchor_scales = held([P, S2], U8, "anchor_scales")
         nc.vector.tensor_copy(anchor_scales[:], tab2_scale_win[:].indirect(anchor_list[:]))
@@ -106,24 +106,26 @@ def tile_list_point_anchor_affinity_kernel(
         nc.vector.tensor_copy(point_scales[:], tab_scale_win[:].indirect(point_list[:]))
         for a in (2, 3):
             nc.sync.dma_start(planes_of[a][0:100, :].bitcast(I32), point_scales[4 * a : 4 * a + 100, :].bitcast(I32))
-        tab_win[3] = load_words(tab_words[3], "slot_a")
+        weight_planes = laid.tile([P, 4 * H], U8, name="weight_planes", align_bytes=64, offset=0)
+        point_words = laid.tile([P, PASSES * S], U32, name="point_words", align_bytes=64, offset=4 * H + T - 128)
 
-        w1_codes, w1_scales = [], []
-        for a in range(W1_PASSES):
-            grouped = held([P, PACK, P, PACK], BF16, "w1_grouped%d" % a)
-            dst = grouped[:].rearrange("p t m j -> p m j t")
-            src = w1_raw[a][:].rearrange("p j (m t) -> p m j t", t=PACK)
-            if a == 0:
-                nc.scalar.copy(dst, src)
-            else:
-                nc.scalar.copy(dst[:, 0 : P // 2], src[:, 0 : P // 2])
-                nc.vector.tensor_copy(dst[:, P // 2 : P], src[:, P // 2 : P])
-            codes = held([P, H], U32, "w1_codes%d" % a)
-            scales = held([P, H], U8, "w1_scales%d" % a)
-            nc.vector.quantize_mx(codes[:].bitcast(FP8X4), scales[:], grouped[:].rearrange("p t m j -> p (t m j)"))
-            w1_codes.append(codes)
-            w1_scales.append(scales)
-        tab2_win = load_words(tab2_words[0], "slot_b")
+        w1_grouped = [held([P, PACK, P, PACK], BF16, "w1_grouped%d" % a) for a in range(W1_PASSES)]
+        w1_codes = [held([P, H], U32, "w1_codes%d" % a) for a in range(W1_PASSES)]
+
+        def round_w1(a):
+            nc.scalar.copy(
+                w1_grouped[a][:].rearrange("p t m j -> p m j t"), w1_raw[a][:].rearrange("p j (m t) -> p m j t", t=PACK)
+            )
+
+        def quantize_w1(a):
+            nc.vector.quantize_mx(
+                w1_codes[a][:].bitcast(FP8X4),
+                weight_planes[:, a * H : (a + 1) * H],
+                w1_grouped[a][:].rearrange("p t m j -> p (t m j)"),
+            )
+
+        round_w1(0)
+        tab_win[2] = load_words(tab_words[2], "slot_a")
 
         turned = bank(4)
         nc.tensor.transpose(turned[:, 0:P], rows[:], identity[:])
@@ -139,16 +141,16 @@ def tile_list_point_anchor_affinity_kernel(
                 )
             nc.scalar.copy(minus_p2[:, half * N : (half + 1) * N], spread[:])
 
-        point_words = {}
+        round_w1(1)
+
+        def picked(a, half):
+            return point_words[:, a * S + half * N : a * S + (half + 1) * N]
 
         def gather_points(a, half):
-            g = held([P, N], U32, "point_words%d_%d" % (a, half))
             cols = slice(half * N // 16, (half + 1) * N // 16)
-            nc.vector.tensor_copy(g[:], tab_win[a][:].bitcast(U32).indirect(point_list[:, cols]))
-            point_words[a, half] = g
+            nc.vector.tensor_copy(picked(a, half), tab_win[a][:].bitcast(U32).indirect(point_list[:, cols]))
 
         w4_codes = held([P, 2, 2 * H], U8, "w4_codes")
-        w4_planes = held([P, 2, H], U8, "w4_planes")
 
         def deal_w4():
             nc.scalar.copy(
@@ -156,7 +158,7 @@ def tile_list_point_anchor_affinity_kernel(
                 w4_raw[:].bitcast(U16).rearrange("p a (m t) -> p a m t", t=PACK),
             )
             nc.vector.tensor_copy(
-                w4_planes[:].rearrange("p a (t m) -> p a m t", t=PACK),
+                weight_planes[:, 2 * H : 4 * H].rearrange("p (a t m) -> p a m t", a=2, t=PACK),
                 w4_scale_raw[:].rearrange("p a (m t) -> p a m t", t=PACK),
             )
 
@@ -167,28 +169,33 @@ def tile_list_point_anchor_affinity_kernel(
             for t in range(PACK):
                 if a < W1_PASSES:
                     lhs = w1_codes[a][:, t * P : (t + 1) * P].bitcast(FP8X4)
-                    lhs_scale = w1_scales[a][:, t * P : (t + 1) * P]
                     rhs_scale = point_scales[4 * a : P, cols]
                 else:
                     lhs = w4_codes[:, a - W1_PASSES, 2 * t * P : 2 * (t + 1) * P].bitcast(FP4X4)
-                    lhs_scale = w4_planes[:, a - W1_PASSES, t * P : (t + 1) * P]
                     rhs_scale = planes_of[a][:, cols]
                 nc.tensor.matmul_mx(
                     h_banks[half][t][:],
                     lhsT=lhs,
-                    lhsT_scale=lhs_scale,
-                    rhs=point_words[a, half][:].bitcast(FP8X4),
+                    lhsT_scale=weight_planes[:, a * H + t * P : a * H + (t + 1) * P],
+                    rhs=picked(a, half).bitcast(FP8X4),
                     rhs_scale=rhs_scale,
-                    start=(a == PASS_ORDER[0]),
-                    stop=(a == PASS_ORDER[-1]),
+                    start=(a == 0),
+                    stop=(a == PASSES - 1),
                 )
 
-        for a in PASS_ORDER:
-            if a == W1_PASSES:
+        for a in range(PASSES):
+            if a == 1:
                 deal_w4()
+                quantize_w1(1)
             for half in range(HALVES):
                 gather_points(a, half)
+                if (a, half) == (0, 0):
+                    quantize_w1(0)
                 project(a, half)
+            if a == 0:
+                tab_win[3] = load_words(tab_words[3], "slot_c")
+            if a == 1:
+                tab2_win = load_words(tab2_words[0], "slot_b")
 
         early_words = held([P, EARLY], U32, "early_words")
         nc.vector.tensor_copy(early_words[:], tab2_win[:].bitcast(U32).indirect(anchor_list[:, 0 : EARLY // 16]))

@@ -27,6 +27,7 @@ ROW_TILES = S2 // P
 QUADS = 4
 BANKS = 8
 EARLY = 768
+P2_RUN = S // P
 
 
 def tile_list_point_anchor_affinity_kernel(
@@ -37,7 +38,6 @@ def tile_list_point_anchor_affinity_kernel(
         lists = ctx.enter_context(tc.tile_pool(name="lists", bufs=1))
         keep = ctx.enter_context(tc.tile_pool(name="keep", bufs=1))
         ring = ctx.enter_context(tc.tile_pool(name="ring", bufs=4))
-        laid = ctx.enter_context(tc.tile_pool(name="laid", bufs=1))
         psum = ctx.enter_context(tc.psum_pool(name="psum", bufs=1))
 
         def bank(b):
@@ -49,28 +49,6 @@ def tile_list_point_anchor_affinity_kernel(
         anchor_list = lists.tile([P, S2 // 16], U16, name="anchor_list")
         point_list = lists.tile([P, S // 16], U16, name="point_list")
         bias = held([P, PACK], F32, "bias")
-        nc.sync.dma_start(anchor_list[:], offs2)
-        nc.sync.dma_start(point_list[:], offs)
-        nc.sync.dma_start(bias[:], b1.rearrange("(p t) -> p t", t=PACK))
-
-        tab2_scale_win = held([P, T], U8, "tab2_scale_win")
-        tab_scale_win = laid.tile([P, T], U8, name="tab_scale_win", align_bytes=64, offset=4 * H - 64)
-        w4_scale_raw = held([P, 2, H], U8, "w4_scale_raw")
-        planes_of = {a: held([P, S], U8, "plane%d" % a) for a in (2, 3)}
-        rows = held([P, P], F32, "rows")
-        nc.vector.memset(tab2_scale_win[:].bitcast(I32), 0)
-        nc.vector.memset(rows[:], 0.0)
-        nc.vector.memset(w4_scale_raw[:].bitcast(I32), 0)
-        for a in (2, 3):
-            nc.vector.memset(planes_of[a][96:P, :].bitcast(I32), 0)
-        nc.gpsimd.memset(tab_scale_win[:].bitcast(I32), 0)
-        identity = held([P, P], F32, "identity")
-        make_identity(nc, identity[:])
-        for q in range(QUADS):
-            nc.gpsimd.dma_start(
-                tab_scale_win[32 * q : 32 * q + 16, :].bitcast(I32),
-                tab_scales[:, 4 * q : 4 * q + 4, :].bitcast(I32),
-            )
 
         def load_words(src, name):
             t = held([P, T], I32, name)
@@ -82,15 +60,35 @@ def tile_list_point_anchor_affinity_kernel(
             nc.sync.dma_start(t[:], w1[a * 512 : (a + 1) * 512, :].rearrange("(p j) c -> p j c", j=PACK))
             return t
 
+        tab2_scale_win = held([P, T], U8, "tab2_scale_win")
+        tab_scale_win = held([P, T], U8, "slot_a")
+        w4_scale_raw = held([P, 2, H], U8, "w4_scale_raw")
+        planes_of = {a: held([P, S], U8, "plane%d" % a) for a in (2, 3)}
+        nc.vector.memset(tab_scale_win[:].bitcast(I32), 0)
+        nc.vector.memset(tab2_scale_win[:].bitcast(I32), 0)
+        nc.vector.memset(w4_scale_raw[:].bitcast(I32), 0)
+        for a in (2, 3):
+            nc.vector.memset(planes_of[a][96:P, :].bitcast(I32), 0)
+        identity = held([P, P], F32, "identity")
+        make_identity(nc, identity[:])
+
+        nc.sync.dma_start(point_list[:], offs)
+        tab_win = {0: load_words(tab_words[0], "tab_win0")}
+        p2_cols = held([P, P2_RUN], F32, "p2_cols")
+        nc.sync.dma_start(p2_cols[:], p2.rearrange("(p c) -> p c", c=P2_RUN))
+        nc.sync.dma_start(anchor_list[:], offs2)
+        for q in range(QUADS):
+            nc.sync.dma_start(
+                tab_scale_win[32 * q : 32 * q + 16, :].bitcast(I32),
+                tab_scales[:, 4 * q : 4 * q + 4, :].bitcast(I32),
+            )
+        w1_raw = [load_w1(0, "slot_c")]
         for q in range(QUADS):
             nc.sync.dma_start(
                 tab2_scale_win[32 * q : 32 * q + 4, :].bitcast(I32), tab2_scales[0, 4 * q : 4 * q + 4, :].bitcast(I32)
             )
-        w1_raw = [load_w1(0, "slot_a")]
-        tab_win = {0: load_words(tab_words[0], "slot_c")}
-        nc.sync.dma_start(rows[0:ROW_TILES, :], a2.rearrange("(c n) -> c n", n=P))
-        nc.sync.dma_start(rows[ROW_TILES : 2 * ROW_TILES, :], p2.rearrange("(c n) -> c n", n=P))
-        w1_raw.append(load_w1(1, "w1_raw1"))
+        w1_raw.append(load_w1(1, "slot_b"))
+        nc.sync.dma_start(bias[:], b1.rearrange("(p t) -> p t", t=PACK))
         w4_raw = held([P, 2, 2 * H], U8, "w4_raw")
         nc.sync.dma_start(w4_raw[:].bitcast(I32), w4_words.bitcast(I32).rearrange("a p w -> p a w"))
         for q in range(QUADS):
@@ -98,16 +96,42 @@ def tile_list_point_anchor_affinity_kernel(
                 w4_scale_raw[32 * q : 32 * q + 4, :, :].bitcast(I32),
                 w4_scales[:, 4 * q : 4 * q + 4, :].bitcast(I32).rearrange("a r e -> r a e"),
             )
-        tab_win[1] = load_words(tab_words[1], "slot_b")
+        tab_win[1] = load_words(tab_words[1], "tab_win1")
 
-        anchor_scales = held([P, S2], U8, "anchor_scales")
-        nc.vector.tensor_copy(anchor_scales[:], tab2_scale_win[:].indirect(anchor_list[:]))
+        minus_p2 = held([P, S], F32, "minus_p2")
+        for u in range(P2_RUN // PACK):
+            spread = bank(6 + u)
+            for c in range(PACK):
+                col = PACK * u + c
+                nc.tensor.transpose(
+                    spread[:, c * P : (c + 1) * P], p2_cols[:, col : col + 1].to_broadcast([P, P]), identity[:]
+                )
+            nc.scalar.activation(
+                minus_p2[:].rearrange("p (k c) -> p k c", c=P2_RUN)[:, :, PACK * u : PACK * (u + 1)],
+                spread[:].rearrange("p (c k) -> p k c", c=PACK),
+                ACT.Copy,
+                scale=-1.0,
+            )
+
+        point_words = held([P, PASSES * S], U32, "point_words")
+
+        def picked(a, half):
+            return point_words[:, a * S + half * N : a * S + (half + 1) * N]
+
+        def gather_points(a, half):
+            cols = slice(half * N // 16, (half + 1) * N // 16)
+            nc.vector.tensor_copy(picked(a, half), tab_win[a][:].bitcast(U32).indirect(point_list[:, cols]))
+
+        for half in range(HALVES):
+            gather_points(0, half)
         point_scales = held([P, S], U8, "point_scales")
         nc.vector.tensor_copy(point_scales[:], tab_scale_win[:].indirect(point_list[:]))
         for a in (2, 3):
             nc.sync.dma_start(planes_of[a][0:100, :].bitcast(I32), point_scales[4 * a : 4 * a + 100, :].bitcast(I32))
-        weight_planes = laid.tile([P, 4 * H], U8, name="weight_planes", align_bytes=64, offset=0)
-        point_words = laid.tile([P, PASSES * S], U32, name="point_words", align_bytes=64, offset=4 * H + T - 128)
+        tab_win[2] = load_words(tab_words[2], "slot_a")
+        anchor_scales = held([P, S2], U8, "anchor_scales")
+        nc.vector.tensor_copy(anchor_scales[:], tab2_scale_win[:].indirect(anchor_list[:]))
+        weight_planes = held([P, 4 * H], U8, "weight_planes")
 
         w1_grouped = [held([P, PACK, P, PACK], BF16, "w1_grouped%d" % a) for a in range(W1_PASSES)]
         w1_codes = [held([P, H], U32, "w1_codes%d" % a) for a in range(W1_PASSES)]
@@ -125,30 +149,11 @@ def tile_list_point_anchor_affinity_kernel(
             )
 
         round_w1(0)
-        tab_win[2] = load_words(tab_words[2], "slot_a")
-
-        turned = bank(4)
-        nc.tensor.transpose(turned[:, 0:P], rows[:], identity[:])
-        minus_cols = held([P, 2 * ROW_TILES], F32, "minus_cols")
-        nc.scalar.activation(minus_cols[:], turned[:, 0 : 2 * ROW_TILES], ACT.Copy, scale=-1.0)
-        minus_p2 = held([P, S], F32, "minus_p2")
-        for half in range(HALVES):
-            spread = bank(5 + half)
-            for c in range(N // P):
-                col = ROW_TILES + half * (N // P) + c
-                nc.tensor.transpose(
-                    spread[:, c * P : (c + 1) * P], minus_cols[:, col : col + 1].to_broadcast([P, P]), identity[:]
-                )
-            nc.scalar.copy(minus_p2[:, half * N : (half + 1) * N], spread[:])
+        tab_win[3] = load_words(tab_words[3], "slot_c")
+        quantize_w1(0)
 
         round_w1(1)
-
-        def picked(a, half):
-            return point_words[:, a * S + half * N : a * S + (half + 1) * N]
-
-        def gather_points(a, half):
-            cols = slice(half * N // 16, (half + 1) * N // 16)
-            nc.vector.tensor_copy(picked(a, half), tab_win[a][:].bitcast(U32).indirect(point_list[:, cols]))
+        tab2_win = load_words(tab2_words[0], "slot_b")
 
         w4_codes = held([P, 2, 2 * H], U8, "w4_codes")
 
@@ -188,14 +193,13 @@ def tile_list_point_anchor_affinity_kernel(
                 deal_w4()
                 quantize_w1(1)
             for half in range(HALVES):
-                gather_points(a, half)
-                if (a, half) == (0, 0):
-                    quantize_w1(0)
+                if a > 0:
+                    gather_points(a, half)
                 project(a, half)
-            if a == 0:
-                tab_win[3] = load_words(tab_words[3], "slot_c")
-            if a == 1:
-                tab2_win = load_words(tab2_words[0], "slot_b")
+            if a == 2:
+                a2_cols = held([P, ROW_TILES], F32, "slot_a")
+                with nc.allow_non_contiguous_dma(reason="one value of a2 for each partition and row tile"):
+                    nc.sync.dma_start(a2_cols[:], a2.rearrange("(c p) -> p c", p=P))
 
         early_words = held([P, EARLY], U32, "early_words")
         nc.vector.tensor_copy(early_words[:], tab2_win[:].bitcast(U32).indirect(anchor_list[:, 0 : EARLY // 16]))
@@ -229,6 +233,8 @@ def tile_list_point_anchor_affinity_kernel(
         nc.vector.tensor_copy(late_words[:], tab2_win[:].bitcast(U32).indirect(anchor_list[:, EARLY // 16 : S2 // 16]))
 
         planes = add_bias(1)
+        minus_cols = held([P, ROW_TILES], F32, "minus_cols")
+        nc.scalar.activation(minus_cols[:], a2_cols[:], ACT.Copy, scale=-1.0)
         grouped = held([P, N, PACK], BF16, "shared1")
         nc.gpsimd.tensor_scalar(grouped[:], planes[:].rearrange("p t n -> p n t"), 1.0, 0.0, ALU.mult, ALU.add)
         quantize_h(grouped, 1, slice(0, N))

@@ -28,6 +28,7 @@ QUADS = 4
 BANKS = 8
 EARLY = 768
 P2_RUN = S // P
+LEAD = 4
 
 
 def tile_list_point_anchor_affinity_kernel(
@@ -37,7 +38,6 @@ def tile_list_point_anchor_affinity_kernel(
     with ExitStack() as ctx:
         lists = ctx.enter_context(tc.tile_pool(name="lists", bufs=1))
         keep = ctx.enter_context(tc.tile_pool(name="keep", bufs=1))
-        ring = ctx.enter_context(tc.tile_pool(name="ring", bufs=4))
         psum = ctx.enter_context(tc.psum_pool(name="psum", bufs=1))
 
         def bank(b):
@@ -237,29 +237,46 @@ def tile_list_point_anchor_affinity_kernel(
         nc.scalar.activation(minus_cols[:], a2_cols[:], ACT.Copy, scale=-1.0)
         grouped = held([P, N, PACK], BF16, "shared1")
         nc.gpsimd.tensor_scalar(grouped[:], planes[:].rearrange("p t n -> p n t"), 1.0, 0.0, ALU.mult, ALU.add)
-        quantize_h(grouped, 1, slice(0, N))
 
         def anchor_words(c):
             if c * P < EARLY:
                 return early_words[:, c * P : (c + 1) * P]
             return late_words[:, c * P - EARLY : (c + 1) * P - EARLY]
 
-        for half in range(HALVES):
+        results = [held([P, S], F32, "result%d" % c) for c in range(ROW_TILES)]
+        turn = [0]
+
+        def tile_of(c, half):
+            anchors = slice(c * P, (c + 1) * P)
             cols = slice(half * N, (half + 1) * N)
-            for c in range(ROW_TILES):
-                anchors = slice(c * P, (c + 1) * P)
-                dots = bank((half * ROW_TILES + c) % BANKS)
-                nc.tensor.matmul_mx(
-                    dots[:],
-                    lhsT=anchor_words(c).bitcast(FP8X4),
-                    lhsT_scale=anchor_scales[:, anchors],
-                    rhs=h_codes[half][:].bitcast(FP8X4),
-                    rhs_scale=h_scales[half][:],
-                    start=True,
-                    stop=True,
-                )
-                exponent = ring.tile([P, N], F32, name="exponent")
-                nc.vector.scalar_tensor_tensor(exponent[:], minus_p2[:, cols], 0.5, dots[:], ALU.mult, ALU.add)
-                result = ring.tile([P, N], F32, name="result", bufs=10)
-                nc.scalar.activation(result[:], exponent[:], ACT.Exp, bias=minus_cols[:, c : c + 1], scale=2.0)
-                nc.sync.dma_start(out[anchors, cols], result[:])
+            dots = bank(turn[0] % BANKS)
+            turn[0] = turn[0] + 1
+            nc.tensor.matmul_mx(
+                dots[:],
+                lhsT=anchor_words(c).bitcast(FP8X4),
+                lhsT_scale=anchor_scales[:, anchors],
+                rhs=h_codes[half][:].bitcast(FP8X4),
+                rhs_scale=h_scales[half][:],
+                start=True,
+                stop=True,
+            )
+            exponent = held([P, N], F32, "exponent%d_%d" % (half, c))
+            nc.vector.scalar_tensor_tensor(exponent[:], minus_p2[:, cols], 0.5, dots[:], ALU.mult, ALU.add)
+            nc.scalar.activation(results[c][:, cols], exponent[:], ACT.Exp, bias=minus_cols[:, c : c + 1], scale=2.0)
+
+        def store(c, cols):
+            nc.sync.dma_start(out[c * P : (c + 1) * P, cols], results[c][:, cols])
+
+        for c in range(LEAD):
+            tile_of(c, 0)
+            store(c, slice(0, N))
+        tile_of(LEAD, 0)
+        quantize_h(grouped, 1, slice(0, N))
+        for c in range(LEAD, ROW_TILES):
+            if c > LEAD:
+                tile_of(c, 0)
+            tile_of(c, 1)
+            store(c, slice(0, S))
+        for c in range(LEAD):
+            tile_of(c, 1)
+            store(c, slice(N, S))

@@ -28,7 +28,7 @@ QUADS = 4
 BANKS = 8
 EARLY = 768
 P2_RUN = S // P
-LEAD = 4
+COVER = 5
 
 
 def tile_list_point_anchor_affinity_kernel(
@@ -265,18 +265,14 @@ def tile_list_point_anchor_affinity_kernel(
             nc.scalar.activation(results[c][:, cols], exponent[:], ACT.Exp, bias=minus_cols[:, c : c + 1], scale=2.0)
 
         def store(c, cols):
-            nc.sync.dma_start(out[c * P : (c + 1) * P, cols], results[c][:, cols])
+            queue = nc.scalar if c % 2 == 1 else nc.sync
+            queue.dma_start(out[c * P : (c + 1) * P, cols], results[c][:, cols])
 
-        for c in range(LEAD):
+        for c in range(ROW_TILES):
             tile_of(c, 0)
             store(c, slice(0, N))
-        tile_of(LEAD, 0)
-        quantize_h(grouped, 1, slice(0, N))
-        for c in range(LEAD, ROW_TILES):
-            if c > LEAD:
-                tile_of(c, 0)
-            tile_of(c, 1)
-            store(c, slice(0, S))
-        for c in range(LEAD):
+            if c == COVER:
+                quantize_h(grouped, 1, slice(0, N))
+        for c in range(ROW_TILES):
             tile_of(c, 1)
             store(c, slice(N, S))

@@ -64,6 +64,8 @@ def tile_list_point_anchor_affinity_kernel(
         tab_scale_win = held([P, T], U8, "slot_a")
         w4_scale_raw = held([P, 2, H], U8, "w4_scale_raw")
         planes_of = {a: held([P, S], U8, "plane%d" % a) for a in (2, 3)}
+        a2_rows = held([P, P], F32, "a2_rows")
+        nc.vector.memset(a2_rows[:], 0.0)
         nc.vector.memset(tab_scale_win[:].bitcast(I32), 0)
         nc.vector.memset(tab2_scale_win[:].bitcast(I32), 0)
         nc.vector.memset(w4_scale_raw[:].bitcast(I32), 0)
@@ -76,13 +78,14 @@ def tile_list_point_anchor_affinity_kernel(
         tab_win = {0: load_words(tab_words[0], "tab_win0")}
         p2_cols = held([P, P2_RUN], F32, "p2_cols")
         nc.sync.dma_start(p2_cols[:], p2.rearrange("(p c) -> p c", c=P2_RUN))
-        nc.sync.dma_start(anchor_list[:], offs2)
+        nc.sync.dma_start(a2_rows[0:ROW_TILES, :], a2.rearrange("(c p) -> c p", p=P))
         for q in range(QUADS):
             nc.sync.dma_start(
                 tab_scale_win[32 * q : 32 * q + 16, :].bitcast(I32),
                 tab_scales[:, 4 * q : 4 * q + 4, :].bitcast(I32),
             )
         w1_raw = [load_w1(0, "slot_c")]
+        nc.sync.dma_start(anchor_list[:], offs2)
         for q in range(QUADS):
             nc.sync.dma_start(
                 tab2_scale_win[32 * q : 32 * q + 4, :].bitcast(I32), tab2_scales[0, 4 * q : 4 * q + 4, :].bitcast(I32)
@@ -112,6 +115,11 @@ def tile_list_point_anchor_affinity_kernel(
                 ACT.Copy,
                 scale=-1.0,
             )
+
+        turned = bank(5)
+        nc.tensor.transpose(turned[:, 0:P], a2_rows[:], identity[:])
+        minus_cols = held([P, ROW_TILES], F32, "minus_cols")
+        nc.scalar.activation(minus_cols[:], turned[:, 0:ROW_TILES], ACT.Copy, scale=-1.0)
 
         point_words = held([P, PASSES * S], U32, "point_words")
 
@@ -196,10 +204,6 @@ def tile_list_point_anchor_affinity_kernel(
                 if a > 0:
                     gather_points(a, half)
                 project(a, half)
-            if a == 2:
-                a2_cols = held([P, ROW_TILES], F32, "slot_a")
-                with nc.allow_non_contiguous_dma(reason="one value of a2 for each partition and row tile"):
-                    nc.sync.dma_start(a2_cols[:], a2.rearrange("(c p) -> p c", p=P))
 
         early_words = held([P, EARLY], U32, "early_words")
         nc.vector.tensor_copy(early_words[:], tab2_win[:].bitcast(U32).indirect(anchor_list[:, 0 : EARLY // 16]))
@@ -233,8 +237,6 @@ def tile_list_point_anchor_affinity_kernel(
         nc.vector.tensor_copy(late_words[:], tab2_win[:].bitcast(U32).indirect(anchor_list[:, EARLY // 16 : S2 // 16]))
 
         planes = add_bias(1)
-        minus_cols = held([P, ROW_TILES], F32, "minus_cols")
-        nc.scalar.activation(minus_cols[:], a2_cols[:], ACT.Copy, scale=-1.0)
         grouped = held([P, N, PACK], BF16, "shared1")
         nc.gpsimd.tensor_scalar(grouped[:], planes[:].rearrange("p t n -> p n t"), 1.0, 0.0, ALU.mult, ALU.add)
 
@@ -265,8 +267,7 @@ def tile_list_point_anchor_affinity_kernel(
             nc.scalar.activation(results[c][:, cols], exponent[:], ACT.Exp, bias=minus_cols[:, c : c + 1], scale=2.0)
 
         def store(c, cols):
-            queue = nc.scalar if c % 2 == 1 else nc.sync
-            queue.dma_start(out[c * P : (c + 1) * P, cols], results[c][:, cols])
+            nc.sync.dma_start(out[c * P : (c + 1) * P, cols], results[c][:, cols])
 
         for c in range(ROW_TILES):
             tile_of(c, 0)

@@ -26,9 +26,10 @@ W1_PASSES = KP // (P * PACK)
 ROW_TILES = S2 // P
 QUADS = 4
 BANKS = 8
-EARLY = 768
-P2_RUN = S // P
+EARLY = 896
 COVER = 5
+NARROW = 2
+RUNS = S // P
 
 
 def tile_list_point_anchor_affinity_kernel(
@@ -64,8 +65,8 @@ def tile_list_point_anchor_affinity_kernel(
         tab_scale_win = held([P, T], U8, "slot_a")
         w4_scale_raw = held([P, 2, H], U8, "w4_scale_raw")
         planes_of = {a: held([P, S], U8, "plane%d" % a) for a in (2, 3)}
-        a2_rows = held([P, P], F32, "a2_rows")
-        nc.vector.memset(a2_rows[:], 0.0)
+        length_rows = held([P, P], F32, "length_rows")
+        nc.vector.memset(length_rows[:], 0.0)
         nc.vector.memset(tab_scale_win[:].bitcast(I32), 0)
         nc.vector.memset(tab2_scale_win[:].bitcast(I32), 0)
         nc.vector.memset(w4_scale_raw[:].bitcast(I32), 0)
@@ -76,9 +77,8 @@ def tile_list_point_anchor_affinity_kernel(
 
         nc.sync.dma_start(point_list[:], offs)
         tab_win = {0: load_words(tab_words[0], "tab_win0")}
-        p2_cols = held([P, P2_RUN], F32, "p2_cols")
-        nc.sync.dma_start(p2_cols[:], p2.rearrange("(p c) -> p c", c=P2_RUN))
-        nc.sync.dma_start(a2_rows[0:ROW_TILES, :], a2.rearrange("(c p) -> c p", p=P))
+        nc.sync.dma_start(length_rows[0:RUNS, :], p2.rearrange("(c p) -> c p", p=P))
+        nc.sync.dma_start(length_rows[RUNS : 2 * RUNS, :], a2.rearrange("(c p) -> c p", p=P))
         for q in range(QUADS):
             nc.sync.dma_start(
                 tab_scale_win[32 * q : 32 * q + 16, :].bitcast(I32),
@@ -101,25 +101,20 @@ def tile_list_point_anchor_affinity_kernel(
             )
         tab_win[1] = load_words(tab_words[1], "tab_win1")
 
-        minus_p2 = held([P, S], F32, "minus_p2")
-        for u in range(P2_RUN // PACK):
-            spread = bank(6 + u)
-            for c in range(PACK):
-                col = PACK * u + c
-                nc.tensor.transpose(
-                    spread[:, c * P : (c + 1) * P], p2_cols[:, col : col + 1].to_broadcast([P, P]), identity[:]
-                )
-            nc.scalar.activation(
-                minus_p2[:].rearrange("p (k c) -> p k c", c=P2_RUN)[:, :, PACK * u : PACK * (u + 1)],
-                spread[:].rearrange("p (c k) -> p k c", c=PACK),
-                ACT.Copy,
-                scale=-1.0,
-            )
-
         turned = bank(5)
-        nc.tensor.transpose(turned[:, 0:P], a2_rows[:], identity[:])
-        minus_cols = held([P, ROW_TILES], F32, "minus_cols")
-        nc.scalar.activation(minus_cols[:], turned[:, 0:ROW_TILES], ACT.Copy, scale=-1.0)
+        nc.tensor.transpose(turned[:, 0:P], length_rows[:], identity[:])
+        minus_lengths = held([P, 2 * RUNS], F32, "minus_lengths")
+        nc.scalar.activation(minus_lengths[:], turned[:, 0 : 2 * RUNS], ACT.Copy, scale=-1.0)
+        minus_cols = minus_lengths[:, RUNS : 2 * RUNS]
+        minus_p2 = held([P, S], F32, "minus_p2")
+        for half in range(HALVES):
+            spread = bank(6 + half)
+            for c in range(PACK):
+                col = PACK * half + c
+                nc.tensor.transpose(
+                    spread[:, c * P : (c + 1) * P], minus_lengths[:, col : col + 1].to_broadcast([P, P]), identity[:]
+                )
+            nc.scalar.copy(minus_p2[:, half * N : (half + 1) * N], spread[:])
 
         point_words = held([P, PASSES * S], U32, "point_words")
 
@@ -230,50 +225,50 @@ def tile_list_point_anchor_affinity_kernel(
                 grouped[i][:].rearrange("p (c i) t -> p c t i", i=4),
                 planes[:, :, parts[i]].rearrange("p t (c i) -> p c t i", i=4),
             )
-        for i in range(2):
-            quantize_h(grouped[i], 0, parts[i])
-
+        quantize_h(grouped[0], 0, parts[0])
         late_words = held([P, S2 - EARLY], U32, "shared0")
         nc.vector.tensor_copy(late_words[:], tab2_win[:].bitcast(U32).indirect(anchor_list[:, EARLY // 16 : S2 // 16]))
-
-        planes = add_bias(1)
-        grouped = held([P, N, PACK], BF16, "shared1")
-        nc.gpsimd.tensor_scalar(grouped[:], planes[:].rearrange("p t n -> p n t"), 1.0, 0.0, ALU.mult, ALU.add)
+        quantize_h(grouped[1], 0, parts[1])
 
         def anchor_words(c):
             if c * P < EARLY:
                 return early_words[:, c * P : (c + 1) * P]
             return late_words[:, c * P - EARLY : (c + 1) * P - EARLY]
 
+        planes = add_bias(1)
+        grouped = held([P, N, PACK], BF16, "shared1")
+        nc.gpsimd.tensor_scalar(grouped[:], planes[:].rearrange("p t n -> p n t"), 1.0, 0.0, ALU.mult, ALU.add)
+
         results = [held([P, S], F32, "result%d" % c) for c in range(ROW_TILES)]
         turn = [0]
 
-        def tile_of(c, half):
+        def tile_of(c, half, part):
             anchors = slice(c * P, (c + 1) * P)
-            cols = slice(half * N, (half + 1) * N)
+            cols = slice(half * N + part.start, half * N + part.stop)
+            width = part.stop - part.start
             dots = bank(turn[0] % BANKS)
             turn[0] = turn[0] + 1
             nc.tensor.matmul_mx(
-                dots[:],
+                dots[:, 0:width],
                 lhsT=anchor_words(c).bitcast(FP8X4),
                 lhsT_scale=anchor_scales[:, anchors],
-                rhs=h_codes[half][:].bitcast(FP8X4),
-                rhs_scale=h_scales[half][:],
+                rhs=h_codes[half][:, part].bitcast(FP8X4),
+                rhs_scale=h_scales[half][:, part],
                 start=True,
                 stop=True,
             )
-            exponent = held([P, N], F32, "exponent%d_%d" % (half, c))
-            nc.vector.scalar_tensor_tensor(exponent[:], minus_p2[:, cols], 0.5, dots[:], ALU.mult, ALU.add)
+            exponent = held([P, width], F32, "exponent%d_%d" % (c, cols.start))
+            nc.vector.scalar_tensor_tensor(exponent[:], minus_p2[:, cols], 0.5, dots[:, 0:width], ALU.mult, ALU.add)
             nc.scalar.activation(results[c][:, cols], exponent[:], ACT.Exp, bias=minus_cols[:, c : c + 1], scale=2.0)
+            nc.sync.dma_start(out[anchors, cols], results[c][:, cols])
 
-        def store(c, cols):
-            nc.sync.dma_start(out[c * P : (c + 1) * P, cols], results[c][:, cols])
-
-        for c in range(ROW_TILES):
-            tile_of(c, 0)
-            store(c, slice(0, N))
+        whole = slice(0, N)
+        for part in parts:
+            for c in range(NARROW):
+                tile_of(c, 0, part)
+        for c in range(NARROW, ROW_TILES):
+            tile_of(c, 0, whole)
             if c == COVER:
-                quantize_h(grouped, 1, slice(0, N))
+                quantize_h(grouped, 1, whole)
         for c in range(ROW_TILES):
-            tile_of(c, 1)
-            store(c, slice(N, S))
+            tile_of(c, 1, whole)

@@ -129,8 +129,11 @@ def tile_list_point_anchor_affinity_kernel(
             gather_points(0, half)
         point_scales = held([P, S], U8, "point_scales")
         nc.vector.tensor_copy(point_scales[:], tab_scale_win[:].indirect(point_list[:]))
-        for a in (2, 3):
+
+        def move_plane(a):
             nc.sync.dma_start(planes_of[a][0:100, :].bitcast(I32), point_scales[4 * a : 4 * a + 100, :].bitcast(I32))
+
+        move_plane(2)
         tab_win[2] = load_words(tab_words[2], "slot_a")
         anchor_scales = held([P, S2], U8, "anchor_scales")
         nc.vector.tensor_copy(anchor_scales[:], tab2_scale_win[:].indirect(anchor_list[:]))
@@ -153,6 +156,7 @@ def tile_list_point_anchor_affinity_kernel(
 
         round_w1(0)
         tab_win[3] = load_words(tab_words[3], "slot_c")
+        move_plane(3)
         quantize_w1(0)
 
         round_w1(1)

@@ -29,6 +29,7 @@ BANKS = 8
 EARLY = 896
 COVER = 5
 NARROW = 2
+WARM = 3
 RUNS = S // P
 
 
@@ -129,6 +130,17 @@ def tile_list_point_anchor_affinity_kernel(
             gather_points(0, half)
         point_scales = held([P, S], U8, "point_scales")
         nc.vector.tensor_copy(point_scales[:], tab_scale_win[:].indirect(point_list[:]))
+
+        for b in range(WARM):
+            nc.tensor.matmul_mx(
+                bank(BANKS - 1)[:],
+                lhsT=picked(0, 1)[:, 0:P].bitcast(FP8X4),
+                lhsT_scale=point_scales[:, N : N + P],
+                rhs=picked(0, 0).bitcast(FP8X4),
+                rhs_scale=point_scales[:, 0:N],
+                start=True,
+                stop=True,
+            )
 
         def move_plane(a):
             nc.sync.dma_start(planes_of[a][0:100, :].bitcast(I32), point_scales[4 * a : 4 * a + 100, :].bitcast(I32))

@@ -64,7 +64,8 @@ def tile_list_point_anchor_affinity_kernel(
 
         tab2_scale_win = held([P, T], U8, "tab2_scale_win")
         tab_scale_win = held([P, T], U8, "slot_a")
-        w4_scale_raw = held([P, 2, H], U8, "w4_scale_raw")
+        w4_scale_raw = held([P, H], U8, "w4_scale_raw")
+        w4_last_plane = held([P, H], U8, "w4_last_plane")
         planes_of = {a: held([P, S], U8, "plane%d" % a) for a in (2, 3)}
         length_rows = held([P, P], F32, "length_rows")
         nc.vector.memset(length_rows[:], 0.0)
@@ -73,6 +74,7 @@ def tile_list_point_anchor_affinity_kernel(
         nc.vector.memset(w4_scale_raw[:].bitcast(I32), 0)
         for a in (2, 3):
             nc.vector.memset(planes_of[a][96:P, :].bitcast(I32), 0)
+        nc.vector.memset(w4_last_plane[96:P, :].bitcast(I32), 0)
         identity = held([P, P], F32, "identity")
         make_identity(nc, identity[:])
 
@@ -92,15 +94,13 @@ def tile_list_point_anchor_affinity_kernel(
                 tab2_scale_win[32 * q : 32 * q + 4, :].bitcast(I32), tab2_scales[0, 4 * q : 4 * q + 4, :].bitcast(I32)
             )
         w1_raw.append(load_w1(1, "slot_b"))
-        nc.sync.dma_start(bias[:], b1.rearrange("(p t) -> p t", t=PACK))
-        w4_raw = held([P, 2, 2 * H], U8, "w4_raw")
-        nc.sync.dma_start(w4_raw[:].bitcast(I32), w4_words.bitcast(I32).rearrange("a p w -> p a w"))
         for q in range(QUADS):
             nc.sync.dma_start(
-                w4_scale_raw[32 * q : 32 * q + 4, :, :].bitcast(I32),
-                w4_scales[:, 4 * q : 4 * q + 4, :].bitcast(I32).rearrange("a r e -> r a e"),
+                w4_scale_raw[32 * q : 32 * q + 8, :].bitcast(I32), w4_scales[:, 4 * q : 4 * q + 4, :].bitcast(I32)
             )
         tab_win[1] = load_words(tab_words[1], "tab_win1")
+        w4_raw = held([P, 2, 2 * H], U8, "w4_raw")
+        nc.sync.dma_start(w4_raw[:].bitcast(I32), w4_words.bitcast(I32).rearrange("a p w -> p a w"))
 
         turned = bank(5)
         nc.tensor.transpose(turned[:, 0:P], length_rows[:], identity[:])
@@ -147,9 +147,10 @@ def tile_list_point_anchor_affinity_kernel(
 
         move_plane(2)
         tab_win[2] = load_words(tab_words[2], "slot_a")
+        nc.sync.dma_start(bias[:], b1.rearrange("(p t) -> p t", t=PACK))
         anchor_scales = held([P, S2], U8, "anchor_scales")
         nc.vector.tensor_copy(anchor_scales[:], tab2_scale_win[:].indirect(anchor_list[:]))
-        weight_planes = held([P, 4 * H], U8, "weight_planes")
+        weight_planes = held([P, 3 * H], U8, "weight_planes")
 
         w1_grouped = [held([P, PACK, P, PACK], BF16, "w1_grouped%d" % a) for a in range(W1_PASSES)]
         w1_codes = [held([P, H], U32, "w1_codes%d" % a) for a in range(W1_PASSES)]
@@ -171,6 +172,11 @@ def tile_list_point_anchor_affinity_kernel(
         move_plane(3)
         quantize_w1(0)
 
+        nc.vector.tensor_copy(
+            weight_planes[:, 2 * H : 3 * H].rearrange("p (t m) -> p m t", t=PACK),
+            w4_scale_raw[:].rearrange("p (m t) -> p m t", t=PACK),
+        )
+        nc.sync.dma_start(w4_last_plane[0:100, :].bitcast(I32), weight_planes[4:104, 2 * H : 3 * H].bitcast(I32))
         round_w1(1)
         tab2_win = load_words(tab2_words[0], "slot_b")
 
@@ -181,15 +187,12 @@ def tile_list_point_anchor_affinity_kernel(
                 w4_codes[:].bitcast(U16).rearrange("p a (t m) -> p a m t", t=PACK),
                 w4_raw[:].bitcast(U16).rearrange("p a (m t) -> p a m t", t=PACK),
             )
-            nc.vector.tensor_copy(
-                weight_planes[:, 2 * H : 4 * H].rearrange("p (a t m) -> p a m t", a=2, t=PACK),
-                w4_scale_raw[:].rearrange("p a (m t) -> p a m t", t=PACK),
-            )
 
         h_banks = [[bank(PACK * half + t) for t in range(PACK)] for half in range(HALVES)]
 
         def project(a, half):
             cols = slice(half * N, (half + 1) * N)
+            planes = w4_last_plane[:] if a == PASSES - 1 else weight_planes[:, a * H : (a + 1) * H]
             for t in range(PACK):
                 if a < W1_PASSES:
                     lhs = w1_codes[a][:, t * P : (t + 1) * P].bitcast(FP8X4)
@@ -200,7 +203,7 @@ def tile_list_point_anchor_affinity_kernel(
                 nc.tensor.matmul_mx(
                     h_banks[half][t][:],
                     lhsT=lhs,
-                    lhsT_scale=weight_planes[:, a * H + t * P : a * H + (t + 1) * P],
+                    lhsT_scale=planes[:, t * P : (t + 1) * P],
                     rhs=picked(a, half).bitcast(FP8X4),
                     rhs_scale=rhs_scale,
                     start=(a == 0),
@@ -242,9 +245,9 @@ def tile_list_point_anchor_affinity_kernel(
                 planes[:, :, parts[i]].rearrange("p t (c i) -> p c t i", i=4),
             )
         quantize_h(grouped[0], 0, parts[0])
+        quantize_h(grouped[1], 0, parts[1])
         late_words = held([P, S2 - EARLY], U32, "shared0")
         nc.vector.tensor_copy(late_words[:], tab2_win[:].bitcast(U32).indirect(anchor_list[:, EARLY // 16 : S2 // 16]))
-        quantize_h(grouped[1], 0, parts[1])
 
         def anchor_words(c):
             if c * P < EARLY:

@@ -30,6 +30,7 @@ EARLY = 896
 COVER = 5
 NARROW = 2
 WARM = 3
+MOVED = 112
 RUNS = S // P
 
 
@@ -70,11 +71,13 @@ def tile_list_point_anchor_affinity_kernel(
         length_rows = held([P, P], F32, "length_rows")
         nc.vector.memset(length_rows[:], 0.0)
         nc.vector.memset(tab_scale_win[:].bitcast(I32), 0)
-        nc.vector.memset(tab2_scale_win[:].bitcast(I32), 0)
         nc.vector.memset(w4_scale_raw[:].bitcast(I32), 0)
+        nc.vector.memset(tab2_scale_win[:].bitcast(I32), 0)
         for a in (2, 3):
             nc.vector.memset(planes_of[a][96:P, :].bitcast(I32), 0)
         nc.vector.memset(w4_last_plane[96:P, :].bitcast(I32), 0)
+        anchor_scales = held([P, S2], U8, "anchor_scales")
+        nc.vector.memset(anchor_scales[:].bitcast(I32), 0)
         identity = held([P, P], F32, "identity")
         make_identity(nc, identity[:])
 
@@ -88,16 +91,13 @@ def tile_list_point_anchor_affinity_kernel(
                 tab_scales[:, 4 * q : 4 * q + 4, :].bitcast(I32),
             )
         w1_raw = [load_w1(0, "slot_c")]
-        nc.sync.dma_start(anchor_list[:], offs2)
-        for q in range(QUADS):
-            nc.sync.dma_start(
-                tab2_scale_win[32 * q : 32 * q + 4, :].bitcast(I32), tab2_scales[0, 4 * q : 4 * q + 4, :].bitcast(I32)
-            )
-        w1_raw.append(load_w1(1, "slot_b"))
         for q in range(QUADS):
             nc.sync.dma_start(
                 w4_scale_raw[32 * q : 32 * q + 8, :].bitcast(I32), w4_scales[:, 4 * q : 4 * q + 4, :].bitcast(I32)
             )
+        w1_raw.append(load_w1(1, "slot_b"))
+        nc.sync.dma_start(anchor_list[:], offs2)
+        nc.sync.dma_start(tab2_scale_win[0:P:8, :].bitcast(I32), tab2_scales[0].bitcast(I32))
         tab_win[1] = load_words(tab_words[1], "tab_win1")
         w4_raw = held([P, 2, 2 * H], U8, "w4_raw")
         nc.sync.dma_start(w4_raw[:].bitcast(I32), w4_words.bitcast(I32).rearrange("a p w -> p a w"))
@@ -143,13 +143,11 @@ def tile_list_point_anchor_affinity_kernel(
             )
 
         def move_plane(a):
-            nc.sync.dma_start(planes_of[a][0:100, :].bitcast(I32), point_scales[4 * a : 4 * a + 100, :].bitcast(I32))
+            nc.sync.dma_start(planes_of[a][0:MOVED, :].bitcast(I32), point_scales[4 * a : 4 * a + MOVED, :].bitcast(I32))
 
         move_plane(2)
         tab_win[2] = load_words(tab_words[2], "slot_a")
         nc.sync.dma_start(bias[:], b1.rearrange("(p t) -> p t", t=PACK))
-        anchor_scales = held([P, S2], U8, "anchor_scales")
-        nc.vector.tensor_copy(anchor_scales[:], tab2_scale_win[:].indirect(anchor_list[:]))
         weight_planes = held([P, 3 * H], U8, "weight_planes")
 
         w1_grouped = [held([P, PACK, P, PACK], BF16, "w1_grouped%d" % a) for a in range(W1_PASSES)]
@@ -168,7 +166,7 @@ def tile_list_point_anchor_affinity_kernel(
             )
 
         round_w1(0)
-        tab_win[3] = load_words(tab_words[3], "slot_c")
+        tab_win[3] = load_words(tab_words[3], "tab_win3")
         move_plane(3)
         quantize_w1(0)
 
@@ -176,9 +174,15 @@ def tile_list_point_anchor_affinity_kernel(
             weight_planes[:, 2 * H : 3 * H].rearrange("p (t m) -> p m t", t=PACK),
             w4_scale_raw[:].rearrange("p (m t) -> p m t", t=PACK),
         )
-        nc.sync.dma_start(w4_last_plane[0:100, :].bitcast(I32), weight_planes[4:104, 2 * H : 3 * H].bitcast(I32))
+        nc.sync.dma_start(
+            w4_last_plane[0:MOVED, :].bitcast(I32), weight_planes[4 : 4 + MOVED, 2 * H : 3 * H].bitcast(I32)
+        )
+        anchor_rows = held([P, S2], U8, "slot_c")
+        nc.vector.tensor_copy(anchor_rows[:], tab2_scale_win[:].indirect(anchor_list[:]))
         round_w1(1)
-        tab2_win = load_words(tab2_words[0], "slot_b")
+        tab2_win = load_words(tab2_words[0], "tab2_win")
+        for r in range(4):
+            nc.sync.dma_start(anchor_scales[r:P:32, :].bitcast(I32), anchor_rows[8 * r : P : 32, :].bitcast(I32))
 
         w4_codes = held([P, 2, 2 * H], U8, "w4_codes")
 

@@ -58,10 +58,11 @@ def tile_list_point_anchor_affinity_kernel(
             nc.sync.dma_start(t[:], src.rearrange("p t i -> p (t i)").bitcast(I32))
             return t
 
-        def load_w1(a, name):
-            t = held([P, PACK, H], F32, name)
-            nc.sync.dma_start(t[:], w1[a * 512 : (a + 1) * 512, :].rearrange("(p j) c -> p j c", j=PACK))
-            return t
+        w1_raw = [held([P, PACK, H], F32, "w1_raw%d" % a) for a in range(W1_PASSES)]
+
+        def load_w1(a, slots):
+            rows = w1[a * 512 : (a + 1) * 512, :].rearrange("(p j) c -> p j c", j=PACK)
+            nc.sync.dma_start(w1_raw[a][:, slots, :], rows[:, slots, :])
 
         tab2_scale_win = held([P, T], U8, "tab2_scale_win")
         tab_scale_win = held([P, T], U8, "slot_a")
@@ -69,10 +70,10 @@ def tile_list_point_anchor_affinity_kernel(
         w4_last_plane = held([P, H], U8, "w4_last_plane")
         planes_of = {a: held([P, S], U8, "plane%d" % a) for a in (2, 3)}
         length_rows = held([P, P], F32, "length_rows")
+        nc.vector.memset(tab2_scale_win[:].bitcast(I32), 0)
         nc.vector.memset(length_rows[:], 0.0)
         nc.vector.memset(tab_scale_win[:].bitcast(I32), 0)
         nc.vector.memset(w4_scale_raw[:].bitcast(I32), 0)
-        nc.vector.memset(tab2_scale_win[:].bitcast(I32), 0)
         for a in (2, 3):
             nc.vector.memset(planes_of[a][96:P, :].bitcast(I32), 0)
         nc.vector.memset(w4_last_plane[96:P, :].bitcast(I32), 0)
@@ -81,26 +82,31 @@ def tile_list_point_anchor_affinity_kernel(
         identity = held([P, P], F32, "identity")
         make_identity(nc, identity[:])
 
+        nc.sync.dma_start(anchor_list[:], offs2)
+        load_w1(0, slice(0, 2))
+        nc.sync.dma_start(tab2_scale_win[0:P:8, :].bitcast(I32), tab2_scales[0].bitcast(I32))
         nc.sync.dma_start(point_list[:], offs)
-        tab_win = {0: load_words(tab_words[0], "tab_win0")}
         nc.sync.dma_start(length_rows[0:RUNS, :], p2.rearrange("(c p) -> c p", p=P))
         nc.sync.dma_start(length_rows[RUNS : 2 * RUNS, :], a2.rearrange("(c p) -> c p", p=P))
+        tab_win = {0: load_words(tab_words[0], "tab_win0")}
+        load_w1(0, slice(2, 4))
         for q in range(QUADS):
             nc.sync.dma_start(
                 tab_scale_win[32 * q : 32 * q + 16, :].bitcast(I32),
                 tab_scales[:, 4 * q : 4 * q + 4, :].bitcast(I32),
             )
-        w1_raw = [load_w1(0, "slot_c")]
+        load_w1(1, slice(0, 4))
         for q in range(QUADS):
             nc.sync.dma_start(
                 w4_scale_raw[32 * q : 32 * q + 8, :].bitcast(I32), w4_scales[:, 4 * q : 4 * q + 4, :].bitcast(I32)
             )
-        w1_raw.append(load_w1(1, "slot_b"))
-        nc.sync.dma_start(anchor_list[:], offs2)
-        nc.sync.dma_start(tab2_scale_win[0:P:8, :].bitcast(I32), tab2_scales[0].bitcast(I32))
         tab_win[1] = load_words(tab_words[1], "tab_win1")
         w4_raw = held([P, 2, 2 * H], U8, "w4_raw")
         nc.sync.dma_start(w4_raw[:].bitcast(I32), w4_words.bitcast(I32).rearrange("a p w -> p a w"))
+        tab_win[2] = load_words(tab_words[2], "tab_win2")
+
+        anchor_rows = held([P, S2], U8, "anchor_rows")
+        nc.vector.tensor_copy(anchor_rows[:], tab2_scale_win[:].indirect(anchor_list[:]))
 
         turned = bank(5)
         nc.tensor.transpose(turned[:, 0:P], length_rows[:], identity[:])
@@ -117,27 +123,28 @@ def tile_list_point_anchor_affinity_kernel(
                 )
             nc.scalar.copy(minus_p2[:, half * N : (half + 1) * N], spread[:])
 
-        point_words = held([P, PASSES * S], U32, "point_words")
+        point_words = {}
 
         def picked(a, half):
-            return point_words[:, a * S + half * N : a * S + (half + 1) * N]
+            return point_words[a, half][:]
 
         def gather_points(a, half):
             cols = slice(half * N // 16, (half + 1) * N // 16)
+            name = "w1_raw0" if (a, half) == (0, 1) else "point_words%d_%d" % (a, half)
+            point_words[a, half] = held([P, N], U32, name)
             nc.vector.tensor_copy(picked(a, half), tab_win[a][:].bitcast(U32).indirect(point_list[:, cols]))
 
-        for half in range(HALVES):
-            gather_points(0, half)
+        gather_points(0, 0)
         point_scales = held([P, S], U8, "point_scales")
         nc.vector.tensor_copy(point_scales[:], tab_scale_win[:].indirect(point_list[:]))
 
         for b in range(WARM):
             nc.tensor.matmul_mx(
                 bank(BANKS - 1)[:],
-                lhsT=picked(0, 1)[:, 0:P].bitcast(FP8X4),
-                lhsT_scale=point_scales[:, N : N + P],
+                lhsT=point_words[0, 0][:, 0:P].bitcast(FP8X4),
+                lhsT_scale=anchor_rows[:, 0:P],
                 rhs=picked(0, 0).bitcast(FP8X4),
-                rhs_scale=point_scales[:, 0:N],
+                rhs_scale=anchor_rows[:, 0:N],
                 start=True,
                 stop=True,
             )
@@ -146,9 +153,8 @@ def tile_list_point_anchor_affinity_kernel(
             nc.sync.dma_start(planes_of[a][0:MOVED, :].bitcast(I32), point_scales[4 * a : 4 * a + MOVED, :].bitcast(I32))
 
         move_plane(2)
-        tab_win[2] = load_words(tab_words[2], "slot_a")
         nc.sync.dma_start(bias[:], b1.rearrange("(p t) -> p t", t=PACK))
-        weight_planes = held([P, 3 * H], U8, "weight_planes")
+        weight_planes = [held([P, H], U8, "weight_plane%d" % a) for a in range(PASSES - 1)] + [w4_last_plane]
 
         w1_grouped = [held([P, PACK, P, PACK], BF16, "w1_grouped%d" % a) for a in range(W1_PASSES)]
         w1_codes = [held([P, H], U32, "w1_codes%d" % a) for a in range(W1_PASSES)]
@@ -161,7 +167,7 @@ def tile_list_point_anchor_affinity_kernel(
         def quantize_w1(a):
             nc.vector.quantize_mx(
                 w1_codes[a][:].bitcast(FP8X4),
-                weight_planes[:, a * H : (a + 1) * H],
+                weight_planes[a][:],
                 w1_grouped[a][:].rearrange("p t m j -> p (t m j)"),
             )
 
@@ -169,16 +175,15 @@ def tile_list_point_anchor_affinity_kernel(
         tab_win[3] = load_words(tab_words[3], "tab_win3")
         move_plane(3)
         quantize_w1(0)
+        gather_points(0, 1)
 
         nc.vector.tensor_copy(
-            weight_planes[:, 2 * H : 3 * H].rearrange("p (t m) -> p m t", t=PACK),
+            weight_planes[2][:].rearrange("p (t m) -> p m t", t=PACK),
             w4_scale_raw[:].rearrange("p (m t) -> p m t", t=PACK),
         )
         nc.sync.dma_start(
-            w4_last_plane[0:MOVED, :].bitcast(I32), weight_planes[4 : 4 + MOVED, 2 * H : 3 * H].bitcast(I32)
+            w4_last_plane[0:MOVED, :].bitcast(I32), weight_planes[2][4 : 4 + MOVED, :].bitcast(I32)
         )
-        anchor_rows = held([P, S2], U8, "slot_c")
-        nc.vector.tensor_copy(anchor_rows[:], tab2_scale_win[:].indirect(anchor_list[:]))
         round_w1(1)
         tab2_win = load_words(tab2_words[0], "tab2_win")
         for r in range(4):
@@ -196,7 +201,6 @@ def tile_list_point_anchor_affinity_kernel(
 
         def project(a, half):
             cols = slice(half * N, (half + 1) * N)
-            planes = w4_last_plane[:] if a == PASSES - 1 else weight_planes[:, a * H : (a + 1) * H]
             for t in range(PACK):
                 if a < W1_PASSES:
                     lhs = w1_codes[a][:, t * P : (t + 1) * P].bitcast(FP8X4)
@@ -207,7 +211,7 @@ def tile_list_point_anchor_affinity_kernel(
                 nc.tensor.matmul_mx(
                     h_banks[half][t][:],
                     lhsT=lhs,
-                    lhsT_scale=planes[:, t * P : (t + 1) * P],
+                    lhsT_scale=weight_planes[a][:, t * P : (t + 1) * P],
                     rhs=picked(a, half).bitcast(FP8X4),
                     rhs_scale=rhs_scale,
                     start=(a == 0),

@@ -66,8 +66,7 @@ def tile_list_point_anchor_affinity_kernel(
 
         tab2_scale_win = held([P, T], U8, "tab2_scale_win")
         tab_scale_win = held([P, T], U8, "slot_a")
-        w4_scale_raw = held([P, H], U8, "w4_scale_raw")
-        w4_last_plane = held([P, H], U8, "w4_last_plane")
+        w4_scale_raw = held([P, 2, H], U8, "w4_scale_raw")
         planes_of = {a: held([P, S], U8, "plane%d" % a) for a in (2, 3)}
         length_rows = held([P, P], F32, "length_rows")
         nc.vector.memset(tab2_scale_win[:].bitcast(I32), 0)
@@ -76,7 +75,6 @@ def tile_list_point_anchor_affinity_kernel(
         nc.vector.memset(w4_scale_raw[:].bitcast(I32), 0)
         for a in (2, 3):
             nc.vector.memset(planes_of[a][96:P, :].bitcast(I32), 0)
-        nc.vector.memset(w4_last_plane[96:P, :].bitcast(I32), 0)
         anchor_scales = held([P, S2], U8, "anchor_scales")
         nc.vector.memset(anchor_scales[:].bitcast(I32), 0)
         identity = held([P, P], F32, "identity")
@@ -98,7 +96,8 @@ def tile_list_point_anchor_affinity_kernel(
         load_w1(1, slice(0, 4))
         for q in range(QUADS):
             nc.sync.dma_start(
-                w4_scale_raw[32 * q : 32 * q + 8, :].bitcast(I32), w4_scales[:, 4 * q : 4 * q + 4, :].bitcast(I32)
+                w4_scale_raw[32 * q : 32 * q + 4, :, :].bitcast(I32),
+                w4_scales[:, 4 * q : 4 * q + 4, :].bitcast(I32).rearrange("a r e -> r a e"),
             )
         tab_win[1] = load_words(tab_words[1], "tab_win1")
         w4_raw = held([P, 2, 2 * H], U8, "w4_raw")
@@ -153,36 +152,34 @@ def tile_list_point_anchor_affinity_kernel(
             nc.sync.dma_start(planes_of[a][0:MOVED, :].bitcast(I32), point_scales[4 * a : 4 * a + MOVED, :].bitcast(I32))
 
         move_plane(2)
-        nc.sync.dma_start(bias[:], b1.rearrange("(p t) -> p t", t=PACK))
-        weight_planes = [held([P, H], U8, "weight_plane%d" % a) for a in range(PASSES - 1)] + [w4_last_plane]
+        weight_planes = held([P, PASSES, H], U8, "weight_planes")
 
         w1_grouped = [held([P, PACK, P, PACK], BF16, "w1_grouped%d" % a) for a in range(W1_PASSES)]
-        w1_codes = [held([P, H], U32, "w1_codes%d" % a) for a in range(W1_PASSES)]
+        w1_codes = {}
 
         def round_w1(a):
             nc.scalar.copy(
                 w1_grouped[a][:].rearrange("p t m j -> p m j t"), w1_raw[a][:].rearrange("p j (m t) -> p m j t", t=PACK)
             )
 
-        def quantize_w1(a):
+        def quantize_w1(a, name):
+            w1_codes[a] = held([P, H], U32, name)
             nc.vector.quantize_mx(
                 w1_codes[a][:].bitcast(FP8X4),
-                weight_planes[a][:],
+                weight_planes[:, a, :],
                 w1_grouped[a][:].rearrange("p t m j -> p (t m j)"),
             )
 
         round_w1(0)
         tab_win[3] = load_words(tab_words[3], "tab_win3")
+        nc.sync.dma_start(bias[:], b1.rearrange("(p t) -> p t", t=PACK))
         move_plane(3)
-        quantize_w1(0)
+        quantize_w1(0, "w1_codes0")
         gather_points(0, 1)
 
         nc.vector.tensor_copy(
-            weight_planes[2][:].rearrange("p (t m) -> p m t", t=PACK),
-            w4_scale_raw[:].rearrange("p (m t) -> p m t", t=PACK),
-        )
-        nc.sync.dma_start(
-            w4_last_plane[0:MOVED, :].bitcast(I32), weight_planes[2][4 : 4 + MOVED, :].bitcast(I32)
+            weight_planes[:, W1_PASSES:PASSES, :].rearrange("p a (t m) -> p a m t", t=PACK),
+            w4_scale_raw[:].rearrange("p a (m t) -> p a m t", t=PACK),
         )
         round_w1(1)
         tab2_win = load_words(tab2_words[0], "tab2_win")
@@ -211,7 +208,7 @@ def tile_list_point_anchor_affinity_kernel(
                 nc.tensor.matmul_mx(
                     h_banks[half][t][:],
                     lhsT=lhs,
-                    lhsT_scale=weight_planes[a][:, t * P : (t + 1) * P],
+                    lhsT_scale=weight_planes[:, a, t * P : (t + 1) * P],
                     rhs=picked(a, half).bitcast(FP8X4),
                     rhs_scale=rhs_scale,
                     start=(a == 0),
@@ -221,7 +218,7 @@ def tile_list_point_anchor_affinity_kernel(
         for a in range(PASSES):
             if a == 1:
                 deal_w4()
-                quantize_w1(1)
+                quantize_w1(1, "w4_scale_raw")
             for half in range(HALVES):
                 if a > 0:
                     gather_points(a, half)

@@ -19,19 +19,22 @@ ALU = mybir.AluOpType
 
 P = 128
 PACK = 4
+K_PASS = P * PACK
 N = 512
-HALVES = S // N
-PASSES = K // (P * PACK)
-W1_PASSES = KP // (P * PACK)
-ROW_TILES = S2 // P
-QUADS = 4
 BANKS = 8
-EARLY = 896
-COVER = 5
-NARROW = 2
-WARM = 3
-MOVED = 112
+QUADS, QUAD = 4, 32
+ROWS = 4
+GROUP = 16
+HALVES = S // N
+PASSES = K // K_PASS
+W1_PASSES = KP // K_PASS
+ROW_TILES = S2 // P
 RUNS = S // P
+PLANE_SPAN = (QUADS - 1) * QUAD + ROWS
+EARLY = 896
+NARROW = 2
+COVER = 5
+WARM = 3
 
 
 def tile_list_point_anchor_affinity_kernel(
@@ -49,111 +52,112 @@ def tile_list_point_anchor_affinity_kernel(
         def held(shape, dtype, name):
             return keep.tile(shape, dtype, name=name, align_bytes=64)
 
-        anchor_list = lists.tile([P, S2 // 16], U16, name="anchor_list")
-        point_list = lists.tile([P, S // 16], U16, name="point_list")
+        anchor_list = lists.tile([P, S2 // GROUP], U16, name="anchor_list")
+        point_list = lists.tile([P, S // GROUP], U16, name="point_list")
         bias = held([P, PACK], F32, "bias")
 
         def load_words(src, name):
-            t = held([P, T], I32, name)
-            nc.sync.dma_start(t[:], src.rearrange("p t i -> p (t i)").bitcast(I32))
-            return t
+            words = held([P, T], I32, name)
+            nc.sync.dma_start(words[:], src.rearrange("p t i -> p (t i)").bitcast(I32))
+            return words
 
         w1_raw = [held([P, PACK, H], F32, "w1_raw%d" % a) for a in range(W1_PASSES)]
 
         def load_w1(a, slots):
-            rows = w1[a * 512 : (a + 1) * 512, :].rearrange("(p j) c -> p j c", j=PACK)
+            rows = w1[a * K_PASS : (a + 1) * K_PASS, :].rearrange("(p j) c -> p j c", j=PACK)
             nc.sync.dma_start(w1_raw[a][:, slots, :], rows[:, slots, :])
 
-        tab2_scale_win = held([P, T], U8, "tab2_scale_win")
-        tab_scale_win = held([P, T], U8, "slot_a")
+        anchor_scale_window = held([P, T], U8, "anchor_scale_window")
+        point_scale_window = held([P, T], U8, "point_scale_window")
         w4_scale_raw = held([P, 2, H], U8, "w4_scale_raw")
-        planes_of = {a: held([P, S], U8, "plane%d" % a) for a in (2, 3)}
+        moved_planes = {a: held([P, S], U8, "moved_plane%d" % a) for a in range(W1_PASSES, PASSES)}
         length_rows = held([P, P], F32, "length_rows")
-        nc.vector.memset(tab2_scale_win[:].bitcast(I32), 0)
+        nc.vector.memset(anchor_scale_window[:].bitcast(I32), 0)
         nc.vector.memset(length_rows[:], 0.0)
-        nc.vector.memset(tab_scale_win[:].bitcast(I32), 0)
+        nc.vector.memset(point_scale_window[:].bitcast(I32), 0)
         nc.vector.memset(w4_scale_raw[:].bitcast(I32), 0)
-        for a in (2, 3):
-            nc.vector.memset(planes_of[a][96:P, :].bitcast(I32), 0)
-        anchor_scales = held([P, S2], U8, "anchor_scales")
-        nc.vector.memset(anchor_scales[:].bitcast(I32), 0)
+        for a in range(W1_PASSES, PASSES):
+            nc.vector.memset(moved_planes[a][P - QUAD : P, :].bitcast(I32), 0)
+        anchor_plane = held([P, S2], U8, "anchor_plane")
+        nc.vector.memset(anchor_plane[:].bitcast(I32), 0)
         identity = held([P, P], F32, "identity")
         make_identity(nc, identity[:])
 
         nc.sync.dma_start(anchor_list[:], offs2)
-        load_w1(0, slice(0, 2))
-        nc.sync.dma_start(tab2_scale_win[0:P:8, :].bitcast(I32), tab2_scales[0].bitcast(I32))
+        load_w1(0, slice(0, PACK // 2))
+        nc.sync.dma_start(anchor_scale_window[0 : P : QUAD // ROWS, :].bitcast(I32), tab2_scales[0].bitcast(I32))
         nc.sync.dma_start(point_list[:], offs)
         nc.sync.dma_start(length_rows[0:RUNS, :], p2.rearrange("(c p) -> c p", p=P))
         nc.sync.dma_start(length_rows[RUNS : 2 * RUNS, :], a2.rearrange("(c p) -> c p", p=P))
-        tab_win = {0: load_words(tab_words[0], "tab_win0")}
-        load_w1(0, slice(2, 4))
+        point_window = {0: load_words(tab_words[0], "point_window0")}
+        load_w1(0, slice(PACK // 2, PACK))
         for q in range(QUADS):
             nc.sync.dma_start(
-                tab_scale_win[32 * q : 32 * q + 16, :].bitcast(I32),
-                tab_scales[:, 4 * q : 4 * q + 4, :].bitcast(I32),
+                point_scale_window[QUAD * q : QUAD * q + PASSES * ROWS, :].bitcast(I32),
+                tab_scales[:, ROWS * q : ROWS * (q + 1), :].bitcast(I32),
             )
-        load_w1(1, slice(0, 4))
+        load_w1(1, slice(0, PACK))
         for q in range(QUADS):
             nc.sync.dma_start(
-                w4_scale_raw[32 * q : 32 * q + 4, :, :].bitcast(I32),
-                w4_scales[:, 4 * q : 4 * q + 4, :].bitcast(I32).rearrange("a r e -> r a e"),
+                w4_scale_raw[QUAD * q : QUAD * q + ROWS, :, :].bitcast(I32),
+                w4_scales[:, ROWS * q : ROWS * (q + 1), :].bitcast(I32).rearrange("a r e -> r a e"),
             )
-        tab_win[1] = load_words(tab_words[1], "tab_win1")
+        point_window[1] = load_words(tab_words[1], "point_window1")
         w4_raw = held([P, 2, 2 * H], U8, "w4_raw")
         nc.sync.dma_start(w4_raw[:].bitcast(I32), w4_words.bitcast(I32).rearrange("a p w -> p a w"))
-        tab_win[2] = load_words(tab_words[2], "tab_win2")
+        point_window[2] = load_words(tab_words[2], "point_window2")
 
         anchor_rows = held([P, S2], U8, "anchor_rows")
-        nc.vector.tensor_copy(anchor_rows[:], tab2_scale_win[:].indirect(anchor_list[:]))
+        nc.vector.tensor_copy(anchor_rows[:], anchor_scale_window[:].indirect(anchor_list[:]))
 
-        turned = bank(5)
+        turned = bank(BANKS - HALVES - 1)
         nc.tensor.transpose(turned[:, 0:P], length_rows[:], identity[:])
         minus_lengths = held([P, 2 * RUNS], F32, "minus_lengths")
         nc.scalar.activation(minus_lengths[:], turned[:, 0 : 2 * RUNS], ACT.Copy, scale=-1.0)
-        minus_cols = minus_lengths[:, RUNS : 2 * RUNS]
+        minus_a2 = minus_lengths[:, RUNS : 2 * RUNS]
         minus_p2 = held([P, S], F32, "minus_p2")
         for half in range(HALVES):
-            spread = bank(6 + half)
-            for c in range(PACK):
-                col = PACK * half + c
+            spread = bank(BANKS - HALVES + half)
+            for c in range(N // P):
+                run = N // P * half + c
                 nc.tensor.transpose(
-                    spread[:, c * P : (c + 1) * P], minus_lengths[:, col : col + 1].to_broadcast([P, P]), identity[:]
+                    spread[:, c * P : (c + 1) * P], minus_lengths[:, run : run + 1].to_broadcast([P, P]), identity[:]
                 )
             nc.scalar.copy(minus_p2[:, half * N : (half + 1) * N], spread[:])
 
         point_words = {}
 
-        def picked(a, half):
-            return point_words[a, half][:]
-
-        def gather_points(a, half):
-            cols = slice(half * N // 16, (half + 1) * N // 16)
-            name = "w1_raw0" if (a, half) == (0, 1) else "point_words%d_%d" % (a, half)
+        def gather_points(a, half, name):
+            entries = slice(half * N // GROUP, (half + 1) * N // GROUP)
             point_words[a, half] = held([P, N], U32, name)
-            nc.vector.tensor_copy(picked(a, half), tab_win[a][:].bitcast(U32).indirect(point_list[:, cols]))
+            nc.vector.tensor_copy(
+                point_words[a, half][:], point_window[a][:].bitcast(U32).indirect(point_list[:, entries])
+            )
 
-        gather_points(0, 0)
+        gather_points(0, 0, "point_words0_0")
         point_scales = held([P, S], U8, "point_scales")
-        nc.vector.tensor_copy(point_scales[:], tab_scale_win[:].indirect(point_list[:]))
+        nc.vector.tensor_copy(point_scales[:], point_scale_window[:].indirect(point_list[:]))
 
-        for b in range(WARM):
+        for warm in range(WARM):
             nc.tensor.matmul_mx(
                 bank(BANKS - 1)[:],
                 lhsT=point_words[0, 0][:, 0:P].bitcast(FP8X4),
                 lhsT_scale=anchor_rows[:, 0:P],
-                rhs=picked(0, 0).bitcast(FP8X4),
+                rhs=point_words[0, 0][:].bitcast(FP8X4),
                 rhs_scale=anchor_rows[:, 0:N],
                 start=True,
                 stop=True,
             )
 
         def move_plane(a):
-            nc.sync.dma_start(planes_of[a][0:MOVED, :].bitcast(I32), point_scales[4 * a : 4 * a + MOVED, :].bitcast(I32))
+            nc.sync.dma_start(
+                moved_planes[a][0:PLANE_SPAN, :].bitcast(I32),
+                point_scales[ROWS * a : ROWS * a + PLANE_SPAN, :].bitcast(I32),
+            )
 
-        move_plane(2)
+        move_plane(W1_PASSES)
+
         weight_planes = held([P, PASSES, H], U8, "weight_planes")
-
         w1_grouped = [held([P, PACK, P, PACK], BF16, "w1_grouped%d" % a) for a in range(W1_PASSES)]
         w1_codes = {}
 
@@ -171,28 +175,25 @@ def tile_list_point_anchor_affinity_kernel(
             )
 
         round_w1(0)
-        tab_win[3] = load_words(tab_words[3], "tab_win3")
+        point_window[PASSES - 1] = load_words(tab_words[PASSES - 1], "point_window3")
         nc.sync.dma_start(bias[:], b1.rearrange("(p t) -> p t", t=PACK))
-        move_plane(3)
+        move_plane(PASSES - 1)
         quantize_w1(0, "w1_codes0")
-        gather_points(0, 1)
+        gather_points(0, 1, "w1_raw0")
 
         nc.vector.tensor_copy(
             weight_planes[:, W1_PASSES:PASSES, :].rearrange("p a (t m) -> p a m t", t=PACK),
             w4_scale_raw[:].rearrange("p a (m t) -> p a m t", t=PACK),
         )
         round_w1(1)
-        tab2_win = load_words(tab2_words[0], "tab2_win")
-        for r in range(4):
-            nc.sync.dma_start(anchor_scales[r:P:32, :].bitcast(I32), anchor_rows[8 * r : P : 32, :].bitcast(I32))
+
+        anchor_window = load_words(tab2_words[0], "anchor_window")
+        for r in range(ROWS):
+            nc.sync.dma_start(
+                anchor_plane[r:P:QUAD, :].bitcast(I32), anchor_rows[QUAD // ROWS * r : P : QUAD, :].bitcast(I32)
+            )
 
         w4_codes = held([P, 2, 2 * H], U8, "w4_codes")
-
-        def deal_w4():
-            nc.scalar.copy(
-                w4_codes[:].bitcast(U16).rearrange("p a (t m) -> p a m t", t=PACK),
-                w4_raw[:].bitcast(U16).rearrange("p a (m t) -> p a m t", t=PACK),
-            )
 
         h_banks = [[bank(PACK * half + t) for t in range(PACK)] for half in range(HALVES)]
 
@@ -200,99 +201,108 @@ def tile_list_point_anchor_affinity_kernel(
             cols = slice(half * N, (half + 1) * N)
             for t in range(PACK):
                 if a < W1_PASSES:
-                    lhs = w1_codes[a][:, t * P : (t + 1) * P].bitcast(FP8X4)
-                    rhs_scale = point_scales[4 * a : P, cols]
+                    codes = w1_codes[a][:, t * P : (t + 1) * P].bitcast(FP8X4)
+                    point_plane = point_scales[ROWS * a : P, cols]
                 else:
-                    lhs = w4_codes[:, a - W1_PASSES, 2 * t * P : 2 * (t + 1) * P].bitcast(FP4X4)
-                    rhs_scale = planes_of[a][:, cols]
+                    codes = w4_codes[:, a - W1_PASSES, 2 * t * P : 2 * (t + 1) * P].bitcast(FP4X4)
+                    point_plane = moved_planes[a][:, cols]
                 nc.tensor.matmul_mx(
                     h_banks[half][t][:],
-                    lhsT=lhs,
+                    lhsT=codes,
                     lhsT_scale=weight_planes[:, a, t * P : (t + 1) * P],
-                    rhs=picked(a, half).bitcast(FP8X4),
-                    rhs_scale=rhs_scale,
+                    rhs=point_words[a, half][:].bitcast(FP8X4),
+                    rhs_scale=point_plane,
                     start=(a == 0),
                     stop=(a == PASSES - 1),
                 )
 
-        for a in range(PASSES):
-            if a == 1:
-                deal_w4()
-                quantize_w1(1, "w4_scale_raw")
+        for half in range(HALVES):
+            project(0, half)
+        nc.scalar.copy(
+            w4_codes[:].bitcast(U16).rearrange("p a (t m) -> p a m t", t=PACK),
+            w4_raw[:].bitcast(U16).rearrange("p a (m t) -> p a m t", t=PACK),
+        )
+        quantize_w1(1, "w4_scale_raw")
+        for a in range(1, PASSES):
             for half in range(HALVES):
-                if a > 0:
-                    gather_points(a, half)
+                gather_points(a, half, "point_words%d_%d" % (a, half))
                 project(a, half)
 
         early_words = held([P, EARLY], U32, "early_words")
-        nc.vector.tensor_copy(early_words[:], tab2_win[:].bitcast(U32).indirect(anchor_list[:, 0 : EARLY // 16]))
+        nc.vector.tensor_copy(
+            early_words[:], anchor_window[:].bitcast(U32).indirect(anchor_list[:, 0 : EARLY // GROUP])
+        )
 
         def add_bias(half):
-            planes = held([P, PACK, N], BF16, "h_planes%d" % half)
+            rounded = held([P, PACK, N], BF16, "h_rounded%d" % half)
             for t in range(PACK):
-                nc.scalar.activation(planes[:, t, :], h_banks[half][t][:], ACT.Identity, bias=bias[:, t : t + 1])
-            return planes
+                nc.scalar.activation(rounded[:, t, :], h_banks[half][t][:], ACT.Identity, bias=bias[:, t : t + 1])
+            return rounded
 
         def quantize_h(grouped, half, cols):
             nc.vector.quantize_mx(
-                h_codes[half][:, cols].bitcast(FP8X4), h_scales[half][:, cols], grouped[:].rearrange("p n t -> p (n t)")
+                h_codes[half][:, cols].bitcast(FP8X4), h_planes[half][:, cols], grouped[:].rearrange("p n t -> p (n t)")
             )
 
         h_codes = [held([P, N], U32, "h_codes%d" % half) for half in range(HALVES)]
-        h_scales = [held([P, N], U8, "h_scales%d" % half) for half in range(HALVES)]
+        h_planes = [held([P, N], U8, "h_plane%d" % half) for half in range(HALVES)]
 
-        planes = add_bias(0)
-        parts = [slice(0, N // 2), slice(N // 2, N)]
-        grouped = [held([P, N // 2, PACK], BF16, "shared%d" % i) for i in range(2)]
-        for i in range(2):
+        first_rounded = add_bias(0)
+        pieces = [slice(0, N // 2), slice(N // 2, N)]
+        first_grouped = [held([P, N // 2, PACK], BF16, "h_grouped%d" % i) for i in range(len(pieces))]
+        for i, piece in enumerate(pieces):
             nc.vector.tensor_copy(
-                grouped[i][:].rearrange("p (c i) t -> p c t i", i=4),
-                planes[:, :, parts[i]].rearrange("p t (c i) -> p c t i", i=4),
+                first_grouped[i][:].rearrange("p (c i) t -> p c t i", i=4),
+                first_rounded[:, :, piece].rearrange("p t (c i) -> p c t i", i=4),
             )
-        quantize_h(grouped[0], 0, parts[0])
-        quantize_h(grouped[1], 0, parts[1])
-        late_words = held([P, S2 - EARLY], U32, "shared0")
-        nc.vector.tensor_copy(late_words[:], tab2_win[:].bitcast(U32).indirect(anchor_list[:, EARLY // 16 : S2 // 16]))
+        for i, piece in enumerate(pieces):
+            quantize_h(first_grouped[i], 0, piece)
+        late_words = held([P, S2 - EARLY], U32, "h_grouped0")
+        nc.vector.tensor_copy(
+            late_words[:], anchor_window[:].bitcast(U32).indirect(anchor_list[:, EARLY // GROUP : S2 // GROUP])
+        )
 
         def anchor_words(c):
             if c * P < EARLY:
                 return early_words[:, c * P : (c + 1) * P]
             return late_words[:, c * P - EARLY : (c + 1) * P - EARLY]
 
-        planes = add_bias(1)
-        grouped = held([P, N, PACK], BF16, "shared1")
-        nc.gpsimd.tensor_scalar(grouped[:], planes[:].rearrange("p t n -> p n t"), 1.0, 0.0, ALU.mult, ALU.add)
+        second_rounded = add_bias(1)
+        second_grouped = held([P, N, PACK], BF16, "h_grouped1")
+        nc.gpsimd.tensor_scalar(
+            second_grouped[:], second_rounded[:].rearrange("p t n -> p n t"), 1.0, 0.0, ALU.mult, ALU.add
+        )
 
         results = [held([P, S], F32, "result%d" % c) for c in range(ROW_TILES)]
-        turn = [0]
+        made = []
 
-        def tile_of(c, half, part):
+        def output_tile(c, half, piece):
             anchors = slice(c * P, (c + 1) * P)
-            cols = slice(half * N + part.start, half * N + part.stop)
-            width = part.stop - part.start
-            dots = bank(turn[0] % BANKS)
-            turn[0] = turn[0] + 1
+            cols = slice(half * N + piece.start, half * N + piece.stop)
+            width = piece.stop - piece.start
+            dots = bank(len(made) % BANKS)
+            made.append(c)
             nc.tensor.matmul_mx(
                 dots[:, 0:width],
                 lhsT=anchor_words(c).bitcast(FP8X4),
-                lhsT_scale=anchor_scales[:, anchors],
-                rhs=h_codes[half][:, part].bitcast(FP8X4),
-                rhs_scale=h_scales[half][:, part],
+                lhsT_scale=anchor_plane[:, anchors],
+                rhs=h_codes[half][:, piece].bitcast(FP8X4),
+                rhs_scale=h_planes[half][:, piece],
                 start=True,
                 stop=True,
             )
             exponent = held([P, width], F32, "exponent%d_%d" % (c, cols.start))
             nc.vector.scalar_tensor_tensor(exponent[:], minus_p2[:, cols], 0.5, dots[:, 0:width], ALU.mult, ALU.add)
-            nc.scalar.activation(results[c][:, cols], exponent[:], ACT.Exp, bias=minus_cols[:, c : c + 1], scale=2.0)
+            nc.scalar.activation(results[c][:, cols], exponent[:], ACT.Exp, bias=minus_a2[:, c : c + 1], scale=2.0)
             nc.sync.dma_start(out[anchors, cols], results[c][:, cols])
 
         whole = slice(0, N)
-        for part in parts:
+        for piece in pieces:
             for c in range(NARROW):
-                tile_of(c, 0, part)
+                output_tile(c, 0, piece)
         for c in range(NARROW, ROW_TILES):
-            tile_of(c, 0, whole)
+            output_tile(c, 0, whole)
             if c == COVER:
-                quantize_h(grouped, 1, whole)
+                quantize_h(second_grouped, 1, whole)
         for c in range(ROW_TILES):
-            tile_of(c, 1, whole)
+            output_tile(c, 1, whole)

from contextlib import ExitStack

import concourse.mybir as mybir
from concourse.masks import make_identity

K, KP, H, T, S, S2 = 2048, 1024, 512, 2048, 1024, 1024
FLOPS = 2 * K * H * S + 2 * H * S2 * S

F32 = mybir.dt.float32
BF16 = mybir.dt.bfloat16
I32 = mybir.dt.int32
U32 = mybir.dt.uint32
U16 = mybir.dt.uint16
U8 = mybir.dt.uint8
FP8X4 = mybir.dt.float8_e4m3fn_x4
FP4X4 = mybir.dt.float4_e2m1fn_x4
ACT = mybir.ActivationFunctionType
ALU = mybir.AluOpType

P = 128
PACK = 4
K_PASS = P * PACK
N = 512
BANKS = 8
QUADS, QUAD = 4, 32
ROWS = 4
GROUP = 16
HALVES = S // N
PASSES = K // K_PASS
W1_PASSES = KP // K_PASS
ROW_TILES = S2 // P
RUNS = S // P
PLANE_SPAN = (QUADS - 1) * QUAD + ROWS
EARLY = 896
NARROW = 2
COVER = 5
WARM = 3


def tile_list_point_anchor_affinity_kernel(
    tc, tab_words, tab_scales, offs, tab2_words, tab2_scales, offs2, w1, w4_words, w4_scales, b1, p2, a2, out
):
    nc = tc.nc
    with ExitStack() as ctx:
        lists = ctx.enter_context(tc.tile_pool(name="lists", bufs=1))
        keep = ctx.enter_context(tc.tile_pool(name="keep", bufs=1))
        psum = ctx.enter_context(tc.psum_pool(name="psum", bufs=1))

        def bank(b):
            return psum.tile([P, N], F32, name="bank%d" % b)

        def held(shape, dtype, name):
            return keep.tile(shape, dtype, name=name, align_bytes=64)

        anchor_list = lists.tile([P, S2 // GROUP], U16, name="anchor_list")
        point_list = lists.tile([P, S // GROUP], U16, name="point_list")
        bias = held([P, PACK], F32, "bias")

        def load_words(src, name):
            words = held([P, T], I32, name)
            nc.sync.dma_start(words[:], src.rearrange("p t i -> p (t i)").bitcast(I32))
            return words

        w1_raw = [held([P, PACK, H], F32, "w1_raw%d" % a) for a in range(W1_PASSES)]

        def load_w1(a, slots):
            rows = w1[a * K_PASS : (a + 1) * K_PASS, :].rearrange("(p j) c -> p j c", j=PACK)
            nc.sync.dma_start(w1_raw[a][:, slots, :], rows[:, slots, :])

        anchor_scale_window = held([P, T], U8, "anchor_scale_window")
        point_scale_window = held([P, T], U8, "point_scale_window")
        w4_scale_raw = held([P, 2, H], U8, "w4_scale_raw")
        moved_planes = {a: held([P, S], U8, "moved_plane%d" % a) for a in range(W1_PASSES, PASSES)}
        length_rows = held([P, P], F32, "length_rows")
        nc.vector.memset(anchor_scale_window[:].bitcast(I32), 0)
        nc.vector.memset(length_rows[:], 0.0)
        nc.vector.memset(point_scale_window[:].bitcast(I32), 0)
        nc.vector.memset(w4_scale_raw[:].bitcast(I32), 0)
        for a in range(W1_PASSES, PASSES):
            nc.vector.memset(moved_planes[a][P - QUAD : P, :].bitcast(I32), 0)
        anchor_plane = held([P, S2], U8, "anchor_plane")
        nc.vector.memset(anchor_plane[:].bitcast(I32), 0)
        identity = held([P, P], F32, "identity")
        make_identity(nc, identity[:])

        nc.sync.dma_start(anchor_list[:], offs2)
        load_w1(0, slice(0, PACK // 2))
        nc.sync.dma_start(anchor_scale_window[0 : P : QUAD // ROWS, :].bitcast(I32), tab2_scales[0].bitcast(I32))
        nc.sync.dma_start(point_list[:], offs)
        nc.sync.dma_start(length_rows[0:RUNS, :], p2.rearrange("(c p) -> c p", p=P))
        nc.sync.dma_start(length_rows[RUNS : 2 * RUNS, :], a2.rearrange("(c p) -> c p", p=P))
        point_window = {0: load_words(tab_words[0], "point_window0")}
        load_w1(0, slice(PACK // 2, PACK))
        for q in range(QUADS):
            nc.sync.dma_start(
                point_scale_window[QUAD * q : QUAD * q + PASSES * ROWS, :].bitcast(I32),
                tab_scales[:, ROWS * q : ROWS * (q + 1), :].bitcast(I32),
            )
        load_w1(1, slice(0, PACK))
        for q in range(QUADS):
            nc.sync.dma_start(
                w4_scale_raw[QUAD * q : QUAD * q + ROWS, :, :].bitcast(I32),
                w4_scales[:, ROWS * q : ROWS * (q + 1), :].bitcast(I32).rearrange("a r e -> r a e"),
            )
        point_window[1] = load_words(tab_words[1], "point_window1")
        w4_raw = held([P, 2, 2 * H], U8, "w4_raw")
        nc.sync.dma_start(w4_raw[:].bitcast(I32), w4_words.bitcast(I32).rearrange("a p w -> p a w"))
        point_window[2] = load_words(tab_words[2], "point_window2")

        anchor_rows = held([P, S2], U8, "anchor_rows")
        nc.vector.tensor_copy(anchor_rows[:], anchor_scale_window[:].indirect(anchor_list[:]))

        turned = bank(BANKS - HALVES - 1)
        nc.tensor.transpose(turned[:, 0:P], length_rows[:], identity[:])
        minus_lengths = held([P, 2 * RUNS], F32, "minus_lengths")
        nc.scalar.activation(minus_lengths[:], turned[:, 0 : 2 * RUNS], ACT.Copy, scale=-1.0)
        minus_a2 = minus_lengths[:, RUNS : 2 * RUNS]
        minus_p2 = held([P, S], F32, "minus_p2")
        for half in range(HALVES):
            spread = bank(BANKS - HALVES + half)
            for c in range(N // P):
                run = N // P * half + c
                nc.tensor.transpose(
                    spread[:, c * P : (c + 1) * P], minus_lengths[:, run : run + 1].to_broadcast([P, P]), identity[:]
                )
            nc.scalar.copy(minus_p2[:, half * N : (half + 1) * N], spread[:])

        point_words = {}

        def gather_points(a, half, name):
            entries = slice(half * N // GROUP, (half + 1) * N // GROUP)
            point_words[a, half] = held([P, N], U32, name)
            nc.vector.tensor_copy(
                point_words[a, half][:], point_window[a][:].bitcast(U32).indirect(point_list[:, entries])
            )

        gather_points(0, 0, "point_words0_0")
        point_scales = held([P, S], U8, "point_scales")
        nc.vector.tensor_copy(point_scales[:], point_scale_window[:].indirect(point_list[:]))

        for warm in range(WARM):
            nc.tensor.matmul_mx(
                bank(BANKS - 1)[:],
                lhsT=point_words[0, 0][:, 0:P].bitcast(FP8X4),
                lhsT_scale=anchor_rows[:, 0:P],
                rhs=point_words[0, 0][:].bitcast(FP8X4),
                rhs_scale=anchor_rows[:, 0:N],
                start=True,
                stop=True,
            )

        def move_plane(a):
            nc.sync.dma_start(
                moved_planes[a][0:PLANE_SPAN, :].bitcast(I32),
                point_scales[ROWS * a : ROWS * a + PLANE_SPAN, :].bitcast(I32),
            )

        move_plane(W1_PASSES)

        weight_planes = held([P, PASSES, H], U8, "weight_planes")
        w1_grouped = [held([P, PACK, P, PACK], BF16, "w1_grouped%d" % a) for a in range(W1_PASSES)]
        w1_codes = {}

        def round_w1(a):
            nc.scalar.copy(
                w1_grouped[a][:].rearrange("p t m j -> p m j t"), w1_raw[a][:].rearrange("p j (m t) -> p m j t", t=PACK)
            )

        def quantize_w1(a, name):
            w1_codes[a] = held([P, H], U32, name)
            nc.vector.quantize_mx(
                w1_codes[a][:].bitcast(FP8X4),
                weight_planes[:, a, :],
                w1_grouped[a][:].rearrange("p t m j -> p (t m j)"),
            )

        round_w1(0)
        point_window[PASSES - 1] = load_words(tab_words[PASSES - 1], "point_window3")
        nc.sync.dma_start(bias[:], b1.rearrange("(p t) -> p t", t=PACK))
        move_plane(PASSES - 1)
        quantize_w1(0, "w1_codes0")
        gather_points(0, 1, "w1_raw0")

        nc.vector.tensor_copy(
            weight_planes[:, W1_PASSES:PASSES, :].rearrange("p a (t m) -> p a m t", t=PACK),
            w4_scale_raw[:].rearrange("p a (m t) -> p a m t", t=PACK),
        )
        round_w1(1)

        anchor_window = load_words(tab2_words[0], "anchor_window")
        for r in range(ROWS):
            nc.sync.dma_start(
                anchor_plane[r:P:QUAD, :].bitcast(I32), anchor_rows[QUAD // ROWS * r : P : QUAD, :].bitcast(I32)
            )

        w4_codes = held([P, 2, 2 * H], U8, "w4_codes")

        h_banks = [[bank(PACK * half + t) for t in range(PACK)] for half in range(HALVES)]

        def project(a, half):
            cols = slice(half * N, (half + 1) * N)
            for t in range(PACK):
                if a < W1_PASSES:
                    codes = w1_codes[a][:, t * P : (t + 1) * P].bitcast(FP8X4)
                    point_plane = point_scales[ROWS * a : P, cols]
                else:
                    codes = w4_codes[:, a - W1_PASSES, 2 * t * P : 2 * (t + 1) * P].bitcast(FP4X4)
                    point_plane = moved_planes[a][:, cols]
                nc.tensor.matmul_mx(
                    h_banks[half][t][:],
                    lhsT=codes,
                    lhsT_scale=weight_planes[:, a, t * P : (t + 1) * P],
                    rhs=point_words[a, half][:].bitcast(FP8X4),
                    rhs_scale=point_plane,
                    start=(a == 0),
                    stop=(a == PASSES - 1),
                )

        for half in range(HALVES):
            project(0, half)
        nc.scalar.copy(
            w4_codes[:].bitcast(U16).rearrange("p a (t m) -> p a m t", t=PACK),
            w4_raw[:].bitcast(U16).rearrange("p a (m t) -> p a m t", t=PACK),
        )
        quantize_w1(1, "w4_scale_raw")
        for a in range(1, PASSES):
            for half in range(HALVES):
                gather_points(a, half, "point_words%d_%d" % (a, half))
                project(a, half)

        early_words = held([P, EARLY], U32, "early_words")
        nc.vector.tensor_copy(
            early_words[:], anchor_window[:].bitcast(U32).indirect(anchor_list[:, 0 : EARLY // GROUP])
        )

        def add_bias(half):
            rounded = held([P, PACK, N], BF16, "h_rounded%d" % half)
            for t in range(PACK):
                nc.scalar.activation(rounded[:, t, :], h_banks[half][t][:], ACT.Identity, bias=bias[:, t : t + 1])
            return rounded

        def quantize_h(grouped, half, cols):
            nc.vector.quantize_mx(
                h_codes[half][:, cols].bitcast(FP8X4), h_planes[half][:, cols], grouped[:].rearrange("p n t -> p (n t)")
            )

        h_codes = [held([P, N], U32, "h_codes%d" % half) for half in range(HALVES)]
        h_planes = [held([P, N], U8, "h_plane%d" % half) for half in range(HALVES)]

        first_rounded = add_bias(0)
        pieces = [slice(0, N // 2), slice(N // 2, N)]
        first_grouped = [held([P, N // 2, PACK], BF16, "h_grouped%d" % i) for i in range(len(pieces))]
        for i, piece in enumerate(pieces):
            nc.vector.tensor_copy(
                first_grouped[i][:].rearrange("p (c i) t -> p c t i", i=4),
                first_rounded[:, :, piece].rearrange("p t (c i) -> p c t i", i=4),
            )
        for i, piece in enumerate(pieces):
            quantize_h(first_grouped[i], 0, piece)
        late_words = held([P, S2 - EARLY], U32, "h_grouped0")
        nc.vector.tensor_copy(
            late_words[:], anchor_window[:].bitcast(U32).indirect(anchor_list[:, EARLY // GROUP : S2 // GROUP])
        )

        def anchor_words(c):
            if c * P < EARLY:
                return early_words[:, c * P : (c + 1) * P]
            return late_words[:, c * P - EARLY : (c + 1) * P - EARLY]

        second_rounded = add_bias(1)
        second_grouped = held([P, N, PACK], BF16, "h_grouped1")
        nc.gpsimd.tensor_scalar(
            second_grouped[:], second_rounded[:].rearrange("p t n -> p n t"), 1.0, 0.0, ALU.mult, ALU.add
        )

        results = [held([P, S], F32, "result%d" % c) for c in range(ROW_TILES)]
        made = []

        def output_tile(c, half, piece):
            anchors = slice(c * P, (c + 1) * P)
            cols = slice(half * N + piece.start, half * N + piece.stop)
            width = piece.stop - piece.start
            dots = bank(len(made) % BANKS)
            made.append(c)
            nc.tensor.matmul_mx(
                dots[:, 0:width],
                lhsT=anchor_words(c).bitcast(FP8X4),
                lhsT_scale=anchor_plane[:, anchors],
                rhs=h_codes[half][:, piece].bitcast(FP8X4),
                rhs_scale=h_planes[half][:, piece],
                start=True,
                stop=True,
            )
            exponent = held([P, width], F32, "exponent%d_%d" % (c, cols.start))
            nc.vector.scalar_tensor_tensor(exponent[:], minus_p2[:, cols], 0.5, dots[:, 0:width], ALU.mult, ALU.add)
            nc.scalar.activation(results[c][:, cols], exponent[:], ACT.Exp, bias=minus_a2[:, c : c + 1], scale=2.0)
            nc.sync.dma_start(out[anchors, cols], results[c][:, cols])

        whole = slice(0, N)
        for piece in pieces:
            for c in range(NARROW):
                output_tile(c, 0, piece)
        for c in range(NARROW, ROW_TILES):
            output_tile(c, 0, whole)
            if c == COVER:
                quantize_h(second_grouped, 1, whole)
        for c in range(ROW_TILES):
            output_tile(c, 1, whole)
